import numpy as np, ml_dtypes
CORES = [40,64,80,88,96,104,120,144]
N = 8
import mx_ref
BF = ml_dtypes.bfloat16
def pick(q, e):
    c = np.concatenate([q[0].reshape(128, -1, 4), np.zeros((128, 1, 4), np.uint8)], axis=1); s = np.concatenate([q[1], np.ones((16, 1), np.uint8)], axis=1)
    return (np.ascontiguousarray(c[:, e].reshape(128, -1)), np.ascontiguousarray(s[:, e]))
def join(*qs):
    return (np.concatenate([q[0] for q in qs], axis=1), np.concatenate([q[1] for q in qs], axis=1))
def put(q, e, v):
    c, s = q[0].reshape(128, -1, 4).copy(), q[1].copy(); c[:, e] = v[0].reshape(128, -1, 4); s[:, e] = v[1]
    return (c.reshape(128, -1), s)
def pk(c, s):
    return (np.ascontiguousarray(c), mx_ref.live(s))
def emit(q):
    return q[0], q[1]
def cols(t, e):
    v = np.concatenate([t.reshape(128, -1, 4), np.zeros((128, 1, 4), BF)], axis=1)
    return np.ascontiguousarray(v[:, e]).reshape(128, -1)
def tile(rs):
    return np.stack(rs, axis=2).reshape(128, -1).astype(BF)
def cut(t, i, w=512):
    return t[:, w * i:w * i + w]
def f(rng, *shape):
    return mx_ref.flush((rng.standard_normal(shape, dtype=np.float32) * np.exp2(rng.integers(-2, 3, shape[:-1] + (1,)))).astype(BF))
def wide(rng, *shape, cols=0):
    v = rng.standard_normal(shape, dtype=np.float32) * np.exp2(rng.integers(-12, 13, shape)).astype(np.float32)
    if cols: v *= np.repeat(np.exp2(rng.integers(-cols, cols + 1, shape[:-2] + (1, shape[-1] // 4))) * (rng.random(shape[:-2] + (1, shape[-1] // 4)) > 0.0625), 4, axis=-1).astype(np.float32)
    return mx_ref.flush(v.astype(BF))
T, CAPP, CB, DF = 128, 32, 16, 64
LEVELS = np.array([0, 16, 32, 64], np.float32)
def taken(first, a):
    return np.concatenate([s * T + np.flatnonzero(first[s] == a)[:CAPP] for s in range(N)])
def plain(rng):
    rt, r2 = np.array(f(rng, 128, 512)), np.zeros((128, 512), BF)
    rt[:, 4 * N:] = 0
    v = f(rng, 128, 4 * N + 4).astype(np.float32).reshape(128, N + 1, 4)
    v = v - np.mean(v, axis=(0, 2), keepdims=True)
    r2[:, :4 * N + 4] = mx_ref.flush(v.reshape(128, -1).astype(BF))
    return {"x": np.array(f(rng, N, 128, 4 * T)), "rt": np.stack([rt] * N), "w": np.array(f(rng, N, 128, 2048)), "r2": np.stack([r2] * N), "vx": f(rng, N, 128, 512), "vh": f(rng, N, 128, 512)}
def planned(rng, A, B, V, dead=None, same=False):
    d = plain(rng)
    rt, r2, wt = d["rt"], d["r2"], d["w"].reshape(N, 128, 4, 128, 4)
    rt[:, 120:] = 0
    r2[:, :4 * N + 4] = 0
    wt[:, 120:] = 0
    for k in range(N + 1):
        r2[:, 4 * k:4 * k + 4, 4 * k:4 * k + 4] = 32
        wt[:, 120 + k // 4, :, 4 * k:4 * k + 4, k % 4] = 64
    k = N + 1
    wt[:, 120 + k // 4, :, :, k % 4] = -64
    if same:
        p = f(rng, 128, 4 * N)
        x = np.stack([cols(p, A[s]) for s in range(N)])
    else: x = f(rng, N, 128, 4 * T)
    x = np.array(x, np.float32).reshape(N, 128, T, 4)
    g = rt[0].astype(np.float32).reshape(128, 128, 4)
    for s in range(N): x[s] = x[s] + g[:, A[s]]
    x[:, 120:] = 0
    s, j = np.nonzero(B >= 0)
    b = B[s, j]
    x[s, 120 + b // 4, j, b % 4] = 64
    x[:, 120 + N // 4, :, N % 4] = LEVELS[V]
    if dead is not None: x[:, 120 + k // 4, :, k % 4] = np.where(dead, 256, 0)
    d["x"] = np.array(mx_ref.flush(x.reshape(N, 128, 4 * T).astype(BF)))
    return d
def choose(rng, A):
    B, V = (A + 1 + rng.integers(0, N - 1, A.shape)) % N, np.zeros((N, T), int)
    for a in range(N):
        k = taken(A, a)
        V.flat[k] = 3
        k = rng.permutation(k)[:DF]
        V.flat[k] = 0
        B.flat[k] = np.resize(rng.permutation([b for b in range(N) if b != a]), len(k))
    return B, V
def setup_inputs(rng):
    return plain(rng)
def setup_inputs_crowd(rng):
    h, A = int(rng.integers(1, N - 1)), []
    o = (int(rng.choice([i for i in range(1, N) if i not in (h, h + 1)])), h)
    for s in range(N):
        one, two, e = (s + o[0]) % N, (s + o[1]) % N, int(rng.integers(1, 9))
        rest = [a for a in range(N) if a not in (one, two, (two + 1) % N)]
        A.append(rng.permutation(np.concatenate([np.full(CAPP, one), np.full(CAPP + e, two), np.resize(rng.permutation(rest), T - 2 * CAPP - e)])))
    A = np.stack(A)
    B, V = choose(rng, A)
    for a in range(N):
        one, two, e = (a + o[0]) % N, (a + o[1]) % N, int(rng.integers(1, CB // 4 + 1))
        rest = [b for b in range(N) if b not in (a, one, two)]
        k = taken(A, a)
        k = rng.permutation(k[V.reshape(-1)[k] == 0])
        B.flat[k] = np.concatenate([np.full(CB, one), np.full(CB + e, two), np.resize(rng.permutation(rest), len(k) - 2 * CB - e)])
    return planned(rng, A, B, V)
def setup_inputs_few(rng):
    none, less, even, full = rng.permutation(N)[:4]
    act, n = [a for a in range(N) if a not in (none, less, even, full)] or [full], DF // (2 * N)
    fix = np.concatenate([np.full(n, less), np.full(2 * n, even), np.full(CAPP + 4, full)])
    A = np.stack([rng.permutation(np.concatenate([fix, np.resize(rng.permutation(act), T - len(fix))])) for s in range(N)])
    B, V = choose(rng, A)
    m = (A == less) | (A == even)
    V[m] = rng.integers(0, 4, int(np.count_nonzero(m)))
    k = taken(A, full)
    V.flat[k] = 3
    k = np.concatenate([k[-16::5], rng.permutation(k[:-16])[:DF - 4]])
    V.flat[k] = 0
    B.flat[k] = np.resize(rng.permutation([b for b in range(N) if b != full]), DF)
    d = planned(rng, A, B, V)
    p, t = 120 + (N + 2) // 4, (N + 2) % 4
    d["x"][:, p, t::4] = 64
    d["w"].reshape(N, 128, 4, 128, 4)[:, p, :, 4 * N + 4:4 * N + 8, t] = 64
    d["r2"][:, 4 * N + 4:4 * N + 8] = 0
    d["r2"][:, 4 * N + 4:4 * N + 8, :4 * N] = -64
    d["x"] = (d["x"].astype(np.float32) * np.float32(2.0 ** 21)).astype(BF)
    d["r2"] = (d["r2"].astype(np.float32) * np.float32(2.0 ** 24)).astype(BF)
    return d
def setup_inputs_ties(rng):
    lo, hi = np.sort(rng.permutation(N)[:2])
    k = int(rng.choice([i for i in range(N - 1) if i != hi]))
    act = [a for a in range(N) if a != hi]
    A = np.stack([rng.permutation(np.resize(rng.permutation(act), T)) for s in range(N)])
    B, V, c = np.zeros((N, T), int), np.full((N, T), 3), 3 * (DF // 6)
    for a in act:
        g = rng.permutation(taken(A, a))
        n = (len(g) - 2 * c) // 3
        B.flat[g] = (a + 1) % N
        V.flat[g[:c]] = 0
        B.flat[g[c:2 * c]] = (a + 2) % N
        V.flat[g[c:2 * c]] = 1
        B.flat[g[2 * c:2 * c + 3 * n]] = (a + 3 + np.repeat(np.arange(n), 3) % (N - 3)) % N
        V.flat[g[2 * c:2 * c + 3 * n]] = 2
    d = planned(rng, A, B, V, same=True)
    d["rt"][:, :, 4 * hi:4 * hi + 4] = d["rt"][:, :, 4 * lo:4 * lo + 4]
    d["r2"][:, 4 * k + 4:4 * k + 8, 4 * k:4 * k + 4] = 32
    d["r2"][:, :, 4 * k + 4:4 * k + 8] = d["r2"][:, :, 4 * k:4 * k + 4]
    return d
def setup_inputs_zero(rng):
    A = np.stack([rng.permutation(np.resize(np.arange(N), T)) for s in range(N)])
    B, V, dead = (A + 1 + rng.integers(0, N - 1, A.shape)) % N, np.full((N, T), 3), np.zeros((N, T), bool)
    for a in range(N):
        k = rng.permutation(taken(A, a))
        z = DF // 2 if a % 2 else DF + DF // 8
        dead.flat[k[:z]] = True
        B.flat[k[:z]] = -1
        V.flat[k[:z]] = 0
        g = k[z:DF]
        if len(g):
            V.flat[g] = 1
            B.flat[g] = np.resize(rng.permutation([b for b in range(N) if b != a]), len(g))
        if a == 0: blank = k[:z:2]
    d = planned(rng, A, B, V, dead=dead)
    nil = np.where(d["rt"][0, :, :4].astype(np.float32) < 0, np.float32(0.0), np.float32(-0.0)).astype(BF)
    for i in blank: d["x"][i // T, :, 4 * (i % T):4 * (i % T) + 4] = nil
    return d
def setup_inputs_spread(rng):
    return {**plain(rng), "x": wide(rng, N, 128, 4 * T, cols=4)}
def check_inputs(d):
    b = []
    for k in ("x", "rt", "w", "r2", "vx", "vh"):
        v = np.abs(d[k].astype(np.float32))
        if not (np.isfinite(v).all() and ((v == 0) | (v >= 2.0 ** -30) & (v <= 2.0 ** 30)).all()): b.append("a value of " + k)
    for k, n in (("rt", N), ("r2", N + 1)):
        v = d[k].astype(np.float32)
        if (v[:, :, 4 * n:] != 0).any(): b.append(k + " has numbers behind its first columns")
        if (v != v[:1]).any(): b.append(k + " differs between ranks")
    return b
def reference(x, rt, w, r2, vx, vh):
    q = [mx_ref.quantize(np.ascontiguousarray(x[s])) for s in range(N)]
    every = join(*q)
    first = np.stack([np.argmax(mx_ref.matmul(mx_ref.quantize(np.ascontiguousarray(rt[s])), q[s])[:N] + np.float32(0.0), axis=0) for s in range(N)])
    who, at, made = np.full((N, N * CB), -1), np.full((N, N * CB), -1), []
    for a in range(N):
        k = taken(first, a)
        t = pick(every, np.concatenate([k, np.full(N * CAPP - len(k), -1)]))
        z = [mx_ref.matmul(mx_ref.quantize(np.ascontiguousarray(cut(w[a], i))), t) for i in range(4)]
        h = mx_ref.quantize(np.ascontiguousarray(tile([np.maximum(v, np.float32(0.0)) * np.float32(0.0625) for v in z])))
        made.append(h)
        e = mx_ref.matmul(mx_ref.quantize(np.ascontiguousarray(r2[a])), h)[:N + 1, :len(k)] + np.float32(0.0)
        late = np.sort(np.argsort(e[N], kind="stable")[:DF])
        e[a] = -np.inf
        second = np.argmax(e[:N], axis=0)
        for b in range(N):
            m = late[second[late] == b][:CB]
            who[b, a * CB:a * CB + len(m)] = k[m]
            at[b, a * CB:a * CB + len(m)] = a * N * CAPP + m
    made = join(*made)
    y, oc, osc = np.zeros((N, 128, N * CB), np.float32), np.zeros((N, 128, 4 * N * CB), np.uint8), np.zeros((N, 16, N * CB), np.uint8)
    for b in range(N):
        t, h = pick(every, who[b]), pick(made, at[b])
        v = mx_ref.matmul(mx_ref.quantize(np.ascontiguousarray(vx[b])), t) + mx_ref.matmul(mx_ref.quantize(np.ascontiguousarray(vh[b])), h)
        y[b] = np.where(who[b] >= 0, v, np.float32(0.0))
        oc[b], osc[b] = emit(h)
    return {"y": y, "who": who.astype(np.float32).reshape(N, 1, N * CB), "oc": oc, "osc": osc}

@@ -1,0 +1,510 @@
+from concourse.bass import DstId, RemoteDMATransfer
+from concourse.mybir import dt, AluOpType, AxisListType, ActivationFunctionType
+
+F8, U8, U16, BF, F32, I32 = "float8_e4m3fn_x4", "uint8", "uint16", "bfloat16", "float32", "int32"
+DF, NR = 64, 8
+NS1, NS2 = 5, 2
+BIG = 1.0e29
+XH_H = 384
+
+
+def _sb(w, d):
+    return ("sbuf", [128, w], d)
+
+
+SCRATCH = {
+    "xt": _sb(512, BF), "rte": _sb(512, BF), "wt": _sb(2048, BF), "r2m": _sb(512, BF), "r2r": _sb(512, BF),
+    "vxt": _sb(512, BF), "vht": _sb(512, BF), "zt": _sb(512, BF), "ht": _sb(1024, BF),
+    "xq": _sb(256, F8), "xs": _sb(256, U8), "rq": _sb(128, F8), "rs": _sb(128, U8), "wq": _sb(512, F8), "ws": _sb(512, U8),
+    "mq": _sb(128, F8), "ms": _sb(128, U8), "eq": _sb(128, F8), "es": _sb(128, U8),
+    "vxq": _sb(128, F8), "vxs": _sb(128, U8), "vhq": _sb(128, F8), "vhs": _sb(128, U8),
+    "s1c": _sb(256, F8), "s1s": _sb(256, U8), "r1c": _sb(128, F8), "r1s": _sb(128, U8), "xh": _sb(768, F8), "xhs": _sb(768, U8),
+    "s2c": _sb(256, F8), "s2s": _sb(256, U8), "r2c": _sb(128, F8), "r2s": _sb(128, U8), "l2c": _sb(272, F8), "l2s": _sb(272, U8),
+    "hp": _sb(128, F8), "hps": _sb(128, U8),
+    "nld": ("dram", [128, 2], BF), "rl1": ("dram", [128, 2], BF), "lnd": ("dram", [8, 128, 2], BF),
+    "wgd": ("dram", [128, 1], F32), "rl2": ("dram", [128, 1], F32), "lwd": ("dram", [8, 128, 1], F32),
+    "p2": _sb(2, I32), "ia": _sb(16, I32), "cf": _sb(16, F32), "of1": _sb(2, U16), "of2": _sb(2, U16), "ofh": _sb(8, U16),
+    "vr": _sb(8, F32), "th1": _sb(8, F32), "th2": _sb(4, F32), "ones": _sb(128, BF), "fix": _sb(128, BF), "zrow": _sb(256, BF),
+    "d0r": _sb(128, F32), "d0": _sb(128, F32), "xa": _sb(32, F32), "xb": _sb(32, F32), "xc": _sb(32, F32), "xd": _sb(32, F32),
+    "mk1": _sb(32, F32), "mk1b": _sb(32, F32), "mk1a": _sb(32, F32), "mk2": _sb(32, F32), "mk2b": _sb(32, F32), "mk2a": _sb(32, F32),
+    "tri": _sb(128, BF), "s128": _sb(256, F32), "bm": _sb(16, F32), "oh32": _sb(8, F32),
+    "t1": _sb(128, F32), "rm": _sb(128, F32), "zb": _sb(144, BF), "oh": _sb(128, BF), "mr": _sb(128, BF), "cum": _sb(128, BF),
+    "js": _sb(1024, BF), "jv": _sb(1024, BF), "l1": _sb(8, F32), "lx1": _sb(32, F32), "lt1": _sb(32, F32), "mn1": _sb(16, F32),
+    "off1": _sb(16, U16), "nlp": _sb(32, BF), "nlt": _sb(32, BF),
+    "nrow": _sb(256, BF), "num": _sb(256, BF), "numt": _sb(256, BF), "tv": _sb(512, BF), "inv": _sb(256, BF),
+    "wn": _sb(272, F32), "vca": _sb(16, F32), "col": _sb(32, F32), "ec": _sb(32, F32), "cc": _sb(512, F32), "lt": _sb(512, BF),
+    "rr": _sb(16, F32), "tvv": _sb(64, BF), "tvt": _sb(64, BF), "rowv": _sb(256, BF), "m2": _sb(256, BF), "cum2": _sb(256, BF),
+    "l2": _sb(8, F32), "lx2": _sb(32, F32), "lt2": _sb(32, F32), "mna": _sb(16, F32), "mn2": _sb(8, F32),
+    "off2": _sb(16, U16), "offw": _sb(8, U16), "wg": _sb(128, F32),
+    "ys": _sb(128, F32),
+    "pw": ("psum", [128, 2048], F32), "pe": ("psum", [128, 1536], F32), "pz": ("psum", [128, 512], F32),
+}
+NDMA = 34
+SEMAPHORES = (["kv", "ks", "kt", "kp", "sent"] + [k + n for k in ("c", "s", "n", "rc", "rs", "rn") for n in "12"]
+              + ["d%d" % i for i in range(NDMA)])
+
+
+def split(engines, parts):
+    k = 1
+    while 2 * k * parts <= len(engines):
+        k *= 2
+    return [engines[k * i:k * i + k] for i in range(parts)]
+
+
+def plan(src, cores, topo):
+    direct = [d for d in cores if d != src and topo.may_write(src, d)]
+    cross = [d for d in cores if d != src and not topo.may_write(src, d)]
+    can = [c for c in topo.cores_of(src) if c != src and all(topo.may_write(c, d) for d in cross)]
+    can.sort(key=lambda c: (topo.die(c) == topo.die(src), c))
+    half = len(cores) // 2
+    helpers = {can[h]: (h, [d for d in cross if cores.index(d) // half == h]) for h in range(2)}
+    p = {"direct": direct, "helpers": helpers, "eng": {}}
+    off = topo.engines(src, direct[0])
+    two = split(off, 4)
+    four = split(off, 2)
+    for i, d in enumerate(direct):
+        p["eng"]["c", d] = two[i]
+        p["eng"]["s", d] = two[3] if i == 0 else four[i - 1]
+        p["eng"]["n", d] = off[i:i + 1]
+    for h in helpers:
+        on = topo.engines(src, h)
+        p["eng"]["c", h] = p["eng"]["s", h] = split(on, 2)[helpers[h][0]]
+        p["eng"]["n", h] = [e for e in on if e not in off][helpers[h][0]:][:1]
+        for i, d in enumerate(helpers[h][1]):
+            e = split(topo.engines(h, d), len(helpers[h][1]))[i]
+            p["eng"]["c", h, d] = p["eng"]["s", h, d] = e
+            p["eng"]["n", h, d] = e[:1]
+    return p
+
+
+def bits(engines):
+    v = 0
+    for e in engines:
+        v |= 1 << e
+    return v
+
+
+def arrivals(kind, core, cores, topo):
+    n = 0
+    for s in cores:
+        if s != core:
+            p = plan(s, cores, topo)
+            if core in p["direct"]:
+                n += len(p["eng"][kind, core])
+            for h in p["helpers"]:
+                if core in p["helpers"][h][1]:
+                    n += len(p["eng"][kind, h, core])
+    return n
+
+
+def transfer(core, to, engines, sem, src, dst, topo):
+    rid, pid = topo.addr(to, core)
+    return RemoteDMATransfer(dst_ids=[DstId(rid=rid, pnc=pid)], dma_engine_mask=bits(engines), remote_sem=sem, src=src, dst=dst)
+
+
+def helper_program(g, core, T, topo):
+    home = [c for c in T.cores if c in topo.cores_of(core)]
+    if not home:
+        return
+    src = home[0]
+    p = plan(src, T.cores, topo)
+    if core not in p["helpers"]:
+        return
+    half, serve = p["helpers"][core]
+    s, sent = T.rank_of(src), 0
+
+    def columns(t, b, w=32):
+        return t[:, w * b:w * b + w]
+
+    for kind, n in (("c", 1), ("n", 1), ("s", 1), ("c", 2), ("s", 2), ("n", 2)):
+        g.wait_ge(T.sem["r%s%d" % (kind, n)], len(p["eng"][kind, core]))
+        tr = []
+        for d in serve:
+            k = T.rank_of(d) % 4
+            if n == 2 and s == 0 and T.rank_of(d) == 1:
+                k = 0
+            if kind == "n":
+                a, b = (T.rl1[:], T.lnd[s]) if n == 1 else (T.rl2[:], T.lwd[s])
+            elif kind == "s":
+                a, b = (columns(T.r1s, k), columns(T.xhs, s)) if n == 1 else (columns(T.r2s, k), columns(T.l2s, s))
+            else:
+                a, b = (columns(T.r1c, k), columns(T.xh, s)) if n == 1 else (columns(T.r2c, k), columns(T.l2c, s))
+                a, b = a.bitcast(dt.uint8), b.bitcast(dt.uint8)
+            tr.append(transfer(core, d, p["eng"][kind, core, d], T.sem["%s%d" % (kind, n)], a, b, topo))
+            sent += len(p["eng"][kind, core, d])
+        g.remote_dma_fused(tr, local_sem=T.sem.sent)
+    g.wait_ge(T.sem.sent, sent)
+
+
+def rank_program(g, core, T, topo):
+    me = T.rank_of(core)
+    if me is None:
+        helper_program(g, core, T, topo)
+        return
+    A, AF = AluOpType, ActivationFunctionType
+    eng = {"v": g.vector, "s": g.scalar, "t": g.tensor, "p": g, "y": g.sync}
+    cnt = {q: 0 for q in eng}
+    seen = {q: {} for q in eng}
+    ndma = [0]
+    everything = {}
+
+    def wait(q, deps):
+        need, todo = {}, list(deps)
+        for d in todo:
+            if isinstance(d, list):
+                todo.extend(d)
+            else:
+                need[d[0]] = max(need.get(d[0], 0), d[1])
+        for sem in need:
+            if seen[q].get(sem, 0) < need[sem]:
+                eng[q].wait_ge(T.sem[sem], need[sem])
+                seen[q][sem] = need[sem]
+
+    def done(q, inst):
+        cnt[q] += 1
+        inst.then_inc(T.sem["k" + q], 1)
+        everything["k" + q] = cnt[q]
+        return ("k" + q, cnt[q])
+
+    def dma(q, out, in_, *deps):
+        wait(q, deps)
+        sem = "d%d" % ndma[0]
+        ndma[0] += 1
+        eng[q].dma_start(out, in_).then_inc(T.sem[sem], 16)
+        everything[sem] = 16
+        return (sem, 16)
+
+    def ts(out, in0, s1, op0, s2, op1, *deps):
+        wait("v", deps)
+        if op1 is None:
+            return done("v", g.vector.tensor_scalar(out, in0, s1, None, op0))
+        return done("v", g.vector.tensor_scalar(out, in0, s1, s2, op0, op1))
+
+    def tt(out, a, b, op, *deps):
+        wait("v", deps)
+        return done("v", g.vector.tensor_tensor(out, a, b, op))
+
+    def copy(out, in_, *deps):
+        wait("v", deps)
+        return done("v", g.vector.tensor_copy(out, in_))
+
+    def fill(ap, c, *deps):
+        wait("v", deps)
+        return done("v", g.vector.memset(ap, c))
+
+    def scan(out, a, b, init, op0, op1, *deps):
+        wait("v", deps)
+        return done("v", g.vector.tensor_tensor_scan(out, a, b, init, op0, op1))
+
+    def turn(out, in_, *deps):
+        wait("v", deps)
+        return done("v", g.vector.transpose(out, in_))
+
+    def total(out, in_, *deps):
+        wait("v", deps)
+        return done("v", g.vector.tensor_reduce(out, in_, AxisListType.X, A.add))
+
+    def quant(q, s, in_, *deps):
+        wait("v", deps)
+        return done("v", g.vector.quantize_mx(q, s, in_))
+
+    def act(out, in_, func, *deps, **kw):
+        wait("s", deps)
+        return done("s", g.scalar.activation(out, in_, func, **kw))
+
+    def mm(out, l, ls, r, rs, start, stop, *deps):
+        wait("t", deps)
+        return done("t", g.tensor.matmul_mx(out, l, ls, r, rs, start, stop))
+
+    def iota(out, pattern, base, cm):
+        return done("p", g.iota(out, pattern, base, cm, allow_small_or_imprecise_dtypes=True))
+
+    ld_x = dma("y", T.xt[:], T.x[:])
+    ld_r = dma("s", T.rte[:, 0:32], T.rt[:, 0:32])
+    ld_w = dma("y", T.wt[:], T.w[:], ld_x)
+    ld_2 = []
+    if me:
+        ld_2.append(dma("y", T.r2m[:, 0:4 * me], T.r2[:, 0:4 * me]))
+        ld_2.append(dma("y", T.r2m[:, 4 * me:4 * me + 4], T.r2[:, 4 * me - 4:4 * me]))
+        ld_2.append(dma("y", T.r2m[:, 4 * me + 4:36], T.r2[:, 4 * me + 4:36]))
+    else:
+        ld_2.append(dma("y", T.r2m[:, 0:4], T.r2[:, 4:8]))
+        ld_2.append(dma("y", T.r2m[:, 4:36], T.r2[:, 4:36]))
+    ld_e = dma("y", T.r2r[:, 0:4], T.r2[:, 32:36])
+    ld_vx = dma("y", T.vxt[:], T.vx[:])
+    ld_vh = dma("y", T.vht[:], T.vh[:])
+    place = {b: (b if me or b != 1 else 0) for b in range(NR)}
+
+    k_p2 = done("p", g.iota(T.p2[:], [[0, 2]], 0, 1))
+    k_d0r = iota(T.d0r[:], [[0, 16], [1, 8]], 0, 0)
+    k_vr = iota(T.vr[:], [[1, 8]], 0, 0)
+    k_xa = iota(T.xa[:], [[0, 2], [1, 2], [0, 8]], 0, 0)
+    k_xb = iota(T.xb[:], [[0, 4], [1, 8]], 0, 0)
+    k_ones = fill(T.ones[:], 1.0)
+    k_zb = fill(T.zb[:], 0.0)
+    k_nlp = fill(T.nlp[:, 16:32], 0.0)
+
+    def bitsof(i, shift, mask):
+        d = T.ia[:, 2 * i:2 * i + 2]
+        wait("v", [k_p2])
+        if shift:
+            return done("v", g.vector.tensor_scalar(d, T.p2[:], shift, mask, A.arith_shift_right, A.bitwise_and))
+        return done("v", g.vector.tensor_scalar(d, T.p2[:], mask, None, A.bitwise_and))
+
+    cf = {n: T.cf[:, i:i + 1] for i, n in enumerate(("a7", "u", "uh", "ul", "blk", "q", "t", "t1", "fx", "t2", "bk4", "b2"))}
+    ka, kuh, kul = bitsof(0, 0, 7), bitsof(2, 4, 1), bitsof(3, 3, 1)
+    k_of1 = copy(T.of1[:], T.ia[:, 0:2], ka)
+    c_a7 = copy(cf["a7"], T.ia[:, 0:1], ka)
+    c_uh = copy(cf["uh"], T.ia[:, 4:5], kuh)
+    c_ul = copy(cf["ul"], T.ia[:, 6:7], kul)
+    c_fx = ts(cf["fx"], cf["a7"], 0.0, A.is_equal, None, None, c_a7)
+    c_t = ts(cf["t"], cf["ul"], 16.0, A.mult, 0.5, A.add, c_ul)
+    k_d0 = ts(T.d0[:], T.d0r[:], 0.0, A.is_equal, -BIG, A.mult, k_d0r)
+    c_t1 = ts(cf["t1"], cf["uh"], 8.0, A.mult, cf["t"], A.add, c_t)
+    k_fix = ts(T.fix[:], T.ones[:], cf["fx"], A.mult, None, None, k_ones, c_fx)
+    k_mk1a = ts(T.mk1a[:], T.xa[:], cf["uh"], A.not_equal, 2000.0, A.mult, k_xa, c_uh)
+    k_mk1b = ts(T.mk1b[:], T.xb[:], NS1 - 0.5, A.is_lt, 128.0, A.mult, k_xb)
+    k_th1 = ts(T.th1[:], T.vr[:], cf["t1"], A.add, None, None, k_vr, c_t1)
+    k_mk1 = tt(T.mk1[:], T.mk1a[:], T.mk1b[:], A.add, k_mk1b)
+
+    t = ld_r
+    for w in (32, 64, 128, 256):
+        t = copy(T.rte[:, w:2 * w], T.rte[:, 0:w], t)
+    q_r = quant(T.rq[:], T.rs[:], T.rte[:], t)
+    k_zt = fill(T.zt[:], 0.0)
+    q_x = quant(T.xq[:, 0:128], T.xs[:, 0:128], T.xt[:], ld_x)
+    m_g = mm(T.pw[:, 0:128], T.rq[:], T.rs[:], T.xq[:, 0:128], T.xs[:, 0:128], True, True, q_x)
+    k_zero1 = quant(T.xq[:, 128:256], T.xs[:, 128:256], T.zt[:], k_zt)
+    v_t1 = turn(T.t1[:], T.pw[:, 0:128], m_g)
+    v_rm = scan(T.rm[:], T.d0[:], T.t1[:], 0.0, A.add, A.max, v_t1, k_d0)
+    for k in range(4):
+        v_z = ts(T.zb[:, 1 + 32 * k:33 + 32 * k], T.rm[:, 32 * k:32 * k + 32], T.rm[:, 32 * k + 7:32 * k + 8], A.is_lt, None, None, v_rm, k_zb)
+    v_oh = tt(T.oh[:], T.zb[:, 0:128], T.zb[:, 1:129], A.subtract, v_z)
+    v_m = turn(T.mr[:], T.oh[:], v_oh)
+    v_c = scan(T.cum[:], T.fix[:], T.mr[:], 0.0, A.add, A.add, v_m, k_fix)
+    acc, part = [], {}
+    for v in range(NS1):
+        acc.append(act(T.js[:, 128 * v:128 * v + 128], T.cum[:], AF.Sign, v_c, k_th1, scale=-1.0, bias=T.th1[:, v:v + 1], accum_out=T.l1[:, v:v + 1]))
+    for v in range(NS1, 8):
+        part[v] = ts(T.jv[:, 128 * v:128 * v + 128], T.cum[:], T.th1[:, v:v + 1], A.is_le, 2.0, A.mult, v_c, k_th1)
+    for v in range(NS1, 8):
+        acc.append(total(T.l1[:, v:v + 1], T.jv[:, 128 * v:128 * v + 128], part[v]))
+    v_lx = tt(T.lx1[:], T.l1[:, 0:8].indirect(T.of1[:, 0:2]), T.mk1[:], A.add, acc, k_mk1, k_of1)
+    v_lt = turn(T.lt1[:], T.lx1[:], v_lx)
+    v_mn = tt(T.mn1[:], T.lt1[:, 0:16], T.lt1[:, 16:32], A.min, v_lt)
+    v_o0 = ts(T.off1[:, 0:16:2], T.mn1[:, 0:8], 0.5, A.mult, None, None, v_mn)
+    v_o1 = ts(T.off1[:, 1:16:2], T.mn1[:, 8:16], 0.5, A.mult, None, None, v_mn)
+    v_s1 = copy(T.s1c[:].bitcast(dt.uint32), T.xq[:].bitcast(dt.uint32).indirect(T.off1[:]), v_o1, v_o0, q_x, k_zero1)
+    a_n0 = act(T.nlp[:, 0:16:2], T.mn1[:, 0:8], AF.Copy, v_mn, scale=0.5)
+    a_n1 = act(T.nlp[:, 1:16:2], T.mn1[:, 8:16], AF.Copy, v_mn, scale=0.5)
+    a_s1 = act(T.s1s[:], T.xs[:].indirect(T.off1[:]), AF.Copy, v_o1)
+    w0 = 32 * me
+    a_own = act(T.xhs[:, w0:w0 + 32], T.xs[:].indirect(T.off1[:, 2 * me:2 * me + 2]), AF.Copy)
+    v_nt = turn(T.nlt[:], T.nlp[:], a_n1, k_nlp)
+    d_nl = dma("y", T.nld[:], T.nlt[0:16, 0:16], v_nt)
+    d_own = dma("y", T.lnd[me], T.nlt[0:16, 0:16])
+    v_own = copy(T.xh[:, w0:w0 + 32].bitcast(dt.uint32), T.xq[:].bitcast(dt.uint32).indirect(T.off1[:, 2 * me:2 * me + 2]))
+
+    p = plan(core, T.cores, topo)
+    sent = [0]
+
+    def send(kind, stage, tos, src_of, dst_of, *deps):
+        wait("p", deps)
+        tr = []
+        for to in tos:
+            e = p["eng"][kind, to]
+            name = kind + stage if to in p["direct"] else "r" + kind + stage
+            tr.append(transfer(core, to, e, T.sem[name], src_of(to), dst_of(to), topo))
+            sent[0] += len(e)
+        g.remote_dma_fused(tr, local_sem=T.sem.sent)
+
+    def send_stage(stage, codes, scales, land_c, land_s, relay_c, relay_s, pl, dep_c, dep_s, numbers, land_n, relay_n, dep_n):
+        def part_of(t, to):
+            if to in p["direct"]:
+                b = pl[T.rank_of(to)]
+                return t[:, 32 * b:32 * b + 32]
+            h = p["helpers"][to][0]
+            return t[:, 128 * h:128 * h + 128]
+
+        def c_src(to):
+            return part_of(codes, to).bitcast(dt.uint8)
+
+        def c_dst(to):
+            return (land_c[:, w0:w0 + 32] if to in p["direct"] else relay_c[:]).bitcast(dt.uint8)
+
+        def s_src(to):
+            return part_of(scales, to)
+
+        def s_dst(to):
+            return land_s[:, w0:w0 + 32] if to in p["direct"] else relay_s[:]
+
+        def n_dst(to):
+            return land_n if to in p["direct"] else relay_n
+
+        hs, ds = sorted(p["helpers"]), p["direct"]
+        send("c", stage, hs, c_src, c_dst, dep_c)
+        send("s", stage, hs, s_src, s_dst, dep_s)
+        send("c", stage, ds, c_src, c_dst)
+        if stage == "1":
+            send("n", stage, hs + ds, lambda to: numbers, n_dst, dep_n)
+        send("s", stage, ds[:1], s_src, s_dst)
+        send("s", stage, ds[1:], s_src, s_dst)
+        if stage == "2":
+            send("n", stage, hs + ds, lambda to: numbers, n_dst, dep_n)
+
+    send_stage("1", T.s1c, T.s1s, T.xh, T.xhs, T.r1c, T.r1s, {b: b for b in range(NR)}, v_s1, a_s1, T.nld[:], T.lnd[me], T.rl1[:], d_nl)
+
+    k_xc = iota(T.xc[:], [[0, 2], [1, 4], [0, 4]], 0, 0)
+    k_xd = iota(T.xd[:], [[0, 8], [1, 4]], 0, 0)
+    k_s128 = iota(T.s128[:], [[128, 8], [0, 32]], 0, 0)
+    k_oh32 = iota(T.oh32[:], [[32, 8]], 16, 0)
+    wait("p", [k_ones])
+    k_tri = done("p", g.affine_select(T.tri[:], T.ones[:], [[-1, 128]], A.is_gt, 0.0, 0, 1))
+    q_w = quant(T.wq[:], T.ws[:], T.wt[:], ld_w)
+    z2 = quant(T.xh[:, 256:384], T.xhs[:, 256:384], T.zt[:])
+    z3 = quant(T.xh[:, 640:768], T.xhs[:, 640:768], T.zt[:])
+    k_tv0 = fill(T.tv[:, 128:256], 0.0)
+    ku, kblk, kq, k3 = bitsof(1, 3, 3), bitsof(4, 5, 3), bitsof(5, 0, 15), bitsof(6, 0, 3)
+    c_u = copy(cf["u"], T.ia[:, 2:3], ku)
+    c_blk = copy(cf["blk"], T.ia[:, 8:9], kblk)
+    c_q = copy(cf["q"], T.ia[:, 10:11], kq)
+    k_of2 = copy(T.of2[:], T.ia[:, 12:14], k3)
+    k_b2 = ts(cf["b2"], cf["a7"], 2.0, A.mult, None, None)
+    c_t2 = ts(cf["t2"], cf["u"], 4.0, A.mult, 0.5, A.add, c_u)
+    c_bk4 = ts(cf["bk4"], cf["blk"], 4.0, A.add, None, None, c_blk)
+    k_bm0 = ts(T.bm[:, 0:8], T.vr[:], cf["blk"], A.is_equal, None, None)
+    k_mk2b = ts(T.mk2b[:], T.xd[:], NS2 - 0.5, A.is_lt, 256.0, A.mult, k_xd)
+    k_mk2a = ts(T.mk2a[:], T.xc[:], cf["u"], A.not_equal, 2000.0, A.mult, k_xc)
+    k_bm1 = ts(T.bm[:, 8:16], T.vr[:], cf["bk4"], A.is_equal, None, None, c_bk4)
+    k_th2 = ts(T.th2[:], T.vr[:, 0:4], cf["t2"], A.add, None, None, c_t2)
+    k_mk2 = tt(T.mk2[:], T.mk2a[:], T.mk2b[:], A.add, k_mk2a)
+    k_ofh = ts(T.ofh[:], T.oh32[:], cf["q"], A.add, None, None, k_oh32, c_q)
+    f_m = fill(T.r2m[:, 64:512], 0.0)
+    f_m2 = fill(T.r2m[:, 36:64], 0.0, ld_2)
+    q_m = quant(T.mq[:], T.ms[:], T.r2m[:], f_m2)
+    t = ld_e
+    for w in (4, 8, 16, 32, 64, 128, 256):
+        t = copy(T.r2r[:, w:2 * w], T.r2r[:, 0:w], t)
+    q_e = quant(T.eq[:], T.es[:], T.r2r[:], t)
+    k_zrow = fill(T.zrow[:], 0.0)
+    k_tvv = fill(T.tvv[:], 0.0)
+    k_wn = fill(T.wn[:, 256:272], -1.0)
+    k_l2 = fill(T.l2[:, 4:8], 0.0)
+    q_vx = quant(T.vxq[:], T.vxs[:], T.vxt[:], ld_vx)
+    q_vh = quant(T.vhq[:], T.vhs[:], T.vht[:], ld_vh)
+    dz = [dma("y", T.l2c[:, w0:w0 + 32].bitcast(dt.uint8), T.xh[:, 256:288].bitcast(dt.uint8), z2),
+          dma("y", T.l2s[:, w0:w0 + 32], T.xhs[:, 256:288]),
+          dma("y", T.l2c[:, 256:272].bitcast(dt.uint8), T.xh[:, 256:272].bitcast(dt.uint8)),
+          dma("y", T.l2s[:, 256:272], T.xhs[:, 256:272])]
+
+    n_c, n_s, n_n = (arrivals(k, core, T.cores, topo) for k in "csn")
+    d_nr = dma("y", T.nrow[0:1, 0:256], T.lnd[:, 16 * me:16 * me + 16, :], ("n1", n_n), d_own)
+    wait("p", [d_nr])
+    g_num = done("p", g.partition_broadcast(T.num[:], T.nrow[0:1, 0:256], 128))
+    ready = [("c1", n_c), ("s1", n_s), v_own, a_own]
+    mw = []
+    for i in range(4):
+        mw.append(mm(T.pw[:, 512 * i:512 * i + 256], T.wq[:, 128 * i:128 * i + 128], T.ws[:, 128 * i:128 * i + 128],
+                     T.xh[:, 0:256], T.xhs[:, 0:256], True, True, q_w, ready, v_t1))
+    col = {n: T.col[:, 2 * i:2 * i + 2] for i, n in enumerate(("num", "inv", "n2", "fe", "sc", "corr", "cc", "A", "F", "F2", "FI", "D", "nI"))}
+    rel = []
+    for i in range(4):
+        o, ps = T.ht[:, i:1024:4], T.pw[:, 512 * i:512 * i + 256]
+        if i % 2 == 0:
+            rel.append(ts(o, ps, 0.0, A.max, 0.0625, A.mult, mw[i]))
+        else:
+            rel.append(act(o, ps, AF.Relu, mw[i], scale=0.0625))
+    q_h = quant(T.xh[:, XH_H:XH_H + 256], T.xhs[:, XH_H:XH_H + 256], T.ht[:], rel)
+    a_va = act(T.inv[:], T.num[:], AF.Sign, g_num, scale=-1.0, bias=127.5, accum_out=T.col[:, 24:25])
+    a_vb = act(T.tv[:, 256:384], T.num[:, 0:128], AF.Sign, scale=-1.0, bias=127.5)
+    v_nt = turn(T.numt[:], T.num[:], g_num)
+    v_ta = tt(T.tv[:, 0:128], T.tri[:], T.inv[:, 0:128], A.mult, a_va, k_tri)
+    v_tb = tt(T.tv[:, 384:512], T.tri[:], T.inv[:, 128:256], A.mult)
+    v_ca = tt(T.vca[:, 0:8], T.numt[:, 0:256:32], T.bm[:, 0:8], A.mult, v_nt, k_bm1)
+    v_cb = tt(T.vca[:, 8:16], T.numt[:, 0:256:32], T.bm[:, 8:16], A.mult)
+    v_ni = ts(T.col[:, 25:26], T.col[:, 24:25], -0.5, A.mult, 128.0, A.add)
+    v_na2 = total(T.col[:, 0:1], T.vca[:, 0:8], v_ca)
+    v_nb2 = total(T.col[:, 1:2], T.vca[:, 8:16], v_cb)
+    v_i16 = ts(col["inv"], col["num"], 127.5, A.is_gt, 32.0, A.mult, v_nb2)
+    for h in range(2):
+        a = XH_H + 128 * h
+        m_e = mm(T.pe[:, 512 * h:512 * h + 128], T.xh[:, a:a + 128], T.xhs[:, a:a + 128], T.mq[:], T.ms[:], True, True, q_h, q_m)
+    m_row = mm(T.pe[:, 1024:1280], T.eq[:], T.es[:], T.xh[:, XH_H:XH_H + 256], T.xhs[:, XH_H:XH_H + 256], True, True, q_e)
+    v_e0 = copy(T.ec[:, 0:16], T.pe[:, 0:16], m_e)
+    v_e1 = copy(T.ec[:, 16:32], T.pe[:, 512:528])
+    e8 = T.ec[:, 8:32:16]
+    f = 0.6 * 2.0 ** -23
+    v_n2 = ts(col["n2"], e8, -f, A.mult, 1e-30, A.max, v_e1)
+    v_fe = ts(col["fe"], e8, f, A.mult, None, None)
+    v_sc = tt(col["sc"], col["fe"], col["n2"], A.max, v_fe)
+    ac = []
+    for h in range(2):
+        ac.append(act(T.cc[:, 256 * h:256 * h + 256], T.tv[:, 256 * h:256 * h + 256], AF.Identity, v_sc, v_tb, a_vb, k_tv0,
+                      scale=T.col[:, 8 + h:9 + h], bias=T.ec[:, 8 + 16 * h:9 + 16 * h]))
+    for h in range(2):
+        v_r = scan(T.rr[:, 8 * h:8 * h + 8], T.d0[:, 0:8], T.ec[:, 16 * h:16 * h + 8], 0.0, A.add, A.max)
+    v_co = ts(col["corr"], e8, 0.0, A.is_gt, T.col[:, 25:26], A.mult, v_ni)
+    v_cc = ts(col["cc"], col["corr"], DF - 0.5, A.add, None, None, v_co)
+    for h in range(2):
+        a_f = act(T.js[:, 512 + 8 * h:520 + 8 * h], T.rr[:, 8 * h:8 * h + 8], AF.Sign, v_r, scale=-1.0, bias=T.rr[:, 8 * h + 7:8 * h + 8], accum_out=T.col[:, 16 + h:17 + h])
+    vl = []
+    for h in range(2):
+        vl.append(tt(T.lt[:, 256 * h:256 * h + 256], T.pe[:, 1024:1280], T.cc[:, 256 * h:256 * h + 256], A.is_lt, ac[h], m_row))
+    a_a = act(T.js[:, 768:1024], T.lt[:, 0:256], AF.Copy, vl[0], accum_out=T.col[:, 14:15])
+    v_f2 = ts(col["F2"], col["F"], 2.0, A.mult, None, None, a_f)
+    v_a1 = total(T.col[:, 15:16], T.lt[:, 256:512], vl[1])
+    v_fi = tt(col["FI"], col["F2"], col["inv"], A.add, v_f2, v_i16)
+    v_d = tt(col["D"], col["A"], col["cc"], A.is_gt, v_a1, a_a, v_cc)
+    v_v = tt(T.tvv[:, 0:64:32], col["FI"], col["D"], A.add, v_d, v_fi, k_tvv)
+    v_tv = turn(T.tvt[:], T.tvv[:], v_v)
+    wait("p", [v_tv])
+    b = [done("p", g.partition_broadcast(T.rowv[:, 64 * q:64 * q + 64], T.tvt[32 * q:32 * q + 1, 0:64], 128)) for q in range(4)]
+    v_wn = tt(T.wn[:, 0:256], T.num[:], T.s128[:], A.add, k_s128)
+    for q in range(4):
+        for h in range(2):
+            v_m2 = ts(T.m2[:, 128 * h + 32 * q:128 * h + 32 * q + 32], T.rowv[:, 64 * q + 32 * h:64 * q + 32 * h + 32], cf["b2"], A.is_equal, None, None, b[q], k_b2)
+    v_c2 = scan(T.cum2[:], T.zrow[:], T.m2[:], 0.0, A.add, A.add, v_m2, k_zrow)
+    acc = []
+    for v in range(NS2):
+        acc.append(act(T.js[:, 256 * v:256 * v + 256], T.cum2[:], AF.Sign, v_c2, k_th2, scale=-1.0, bias=T.th2[:, v:v + 1], accum_out=T.l2[:, v:v + 1]))
+    for v in range(NS2, 4):
+        part[v] = ts(T.jv[:, 256 * v:256 * v + 256], T.cum2[:], T.th2[:, v:v + 1], A.is_le, 2.0, A.mult, v_c2, v_lx)
+    for v in range(NS2, 4):
+        acc.append(total(T.l2[:, v:v + 1], T.jv[:, 256 * v:256 * v + 256], part[v]))
+    v_lx = tt(T.lx2[:], T.l2[:, 0:8].indirect(T.of2[:, 0:2]), T.mk2[:], A.add, acc, k_mk2, k_of2, k_l2)
+    v_lt = turn(T.lt2[:], T.lx2[:], v_lx)
+    v_ma = tt(T.mna[:], T.lt2[:, 0:16], T.lt2[:, 16:32], A.min, v_lt)
+    v_mn = tt(T.mn2[:], T.mna[:, 0:8], T.mna[:, 8:16], A.min, v_ma)
+    v_o0 = ts(T.off2[:, 0:16:2], T.mn2[:], 0.5, A.mult, None, None, v_mn)
+    v_o1 = ts(T.off2[:, 1:16:2], T.mn2[:], 0.5, A.mult, float(XH_H), A.add, v_mn)
+    v_s2 = copy(T.s2c[:].bitcast(dt.uint32), T.xh[:].bitcast(dt.uint32).indirect(T.off2[:]), v_o0, v_o1, ready, q_h, z2, z3)
+    a_s2 = act(T.s2s[:], T.xhs[:].indirect(T.off2[:]), AF.Copy, v_o1, ready)
+    v_ow = ts(T.offw[:], T.mn2[:], 0.5, A.mult, None, None)
+    v_wg = copy(T.wg[:], T.wn[:].indirect(T.offw[:]), v_ow, v_wn, k_wn)
+    runs = [(0, 0, 128)] if me else [(0, 16, 16), (16, 0, 16), (32, 32, 96)]
+    d_wg, d_wo = [], []
+    for to, fr, n in runs:
+        d_wg.append(dma("y", T.wgd[to:to + n, 0], T.wg[0:1, fr:fr + n], v_wg))
+        d_wo.append(dma("s", T.lwd[me, to:to + n, 0], T.wg[0:1, fr:fr + n], v_wg))
+    send_stage("2", T.s2c, T.s2s, T.l2c, T.l2s, T.r2c, T.r2s, place, v_s2, a_s2, T.wgd[:], T.lwd[me], T.rl2[:], d_wg)
+
+    ready = [("c2", n_c), ("s2", n_s), dz]
+    out = (T.pz[:, 0:128], T.pw[:, 512:640])
+    my = []
+    for k in range(2):
+        a = 128 * k
+        mm(out[k], T.vxq[:], T.vxs[:], T.l2c[:, a:a + 128], T.l2s[:, a:a + 128], True, False, ready, q_vx, q_vh, rel)
+        my.append(mm(out[k], T.vhq[:], T.vhs[:], T.l2c[:, a + 16:a + 144], T.l2s[:, a + 16:a + 144], False, True))
+    v_hp = copy(T.hp[:].bitcast(dt.uint32), T.l2c[:, 0:256].bitcast(dt.uint32).indirect(T.ofh[:]), ready, k_ofh)
+    a_hp = act(T.hps[:], T.l2s[:, 0:256].indirect(T.ofh[:]), AF.Copy, ready, k_ofh)
+    dma("y", T.oc[:, 0:512], T.hp[:].bitcast(dt.uint8), v_hp)
+    for i in range(4):
+        v_y = copy(T.ys[:, 16 * i:16 * i + 16], T.pz[:, 32 * i:32 * i + 16], my[0])
+        a_y = act(T.ys[:, 64 + 16 * i:80 + 16 * i], T.pw[:, 512 + 32 * i:528 + 32 * i], AF.Copy, my[1])
+    dma("s", T.y[:, 64:128], T.ys[:, 64:128], a_y)
+    dma("y", T.y[:, 0:64], T.ys[:, 0:64], v_y)
+    for k in range(4):
+        dma("s" if k % 2 else "y", T.osc[4 * k:4 * k + 4, 0:128], T.hps[32 * k:32 * k + 4, 0:128], a_hp)
+    dma("y", T.who[0:1, 0:128], T.lwd[:, 16 * me:16 * me + 16, 0], ("n2", n_n), d_wo)
+    g.wait_ge(T.sem.sent, sent[0])
+    wait("p", [(s, everything[s]) for s in everything])

@@ -3,7 +3,7 @@ from concourse.mybir import dt, AluOpType, AxisListType, ActivationFunctionType
 
 F8, U8, U16, BF, F32, I32 = "float8_e4m3fn_x4", "uint8", "uint16", "bfloat16", "float32", "int32"
 DF, NR = 64, 8
-NS1, NS2 = 5, 2
+NS1, NS2 = 5, 3
 BIG = 1.0e29
 XH_H = 384
 
@@ -25,17 +25,17 @@ SCRATCH = {
     "wgd": ("dram", [128, 1], F32), "rl2": ("dram", [128, 1], F32), "lwd": ("dram", [8, 128, 1], F32),
     "p2": _sb(2, I32), "ia": _sb(16, I32), "cf": _sb(16, F32), "of1": _sb(2, U16), "of2": _sb(2, U16), "ofh": _sb(8, U16),
     "vr": _sb(8, F32), "th1": _sb(8, F32), "th2": _sb(4, F32), "ones": _sb(128, BF), "fix": _sb(128, BF), "zrow": _sb(256, BF),
-    "d0r": _sb(128, F32), "d0": _sb(128, F32), "xa": _sb(32, F32), "xb": _sb(32, F32), "xc": _sb(32, F32), "xd": _sb(32, F32),
-    "mk1": _sb(32, F32), "mk1b": _sb(32, F32), "mk1a": _sb(32, F32), "mk2": _sb(32, F32), "mk2b": _sb(32, F32), "mk2a": _sb(32, F32),
-    "tri": _sb(128, BF), "s128": _sb(256, F32), "bm": _sb(16, F32), "oh32": _sb(8, F32),
+    "d0r": _sb(128, F32), "d0": _sb(128, F32), "xa": _sb(32, F32), "xb": _sb(32, F32),
+    "mk1": _sb(32, F32), "mk1b": _sb(32, F32), "mk1a": _sb(32, F32), "mk2": _sb(32, F32),
+    "c127": _sb(128, BF), "tri": _sb(128, BF), "s128": _sb(256, F32), "oh32": _sb(8, F32),
     "t1": _sb(128, F32), "rm": _sb(128, F32), "zb": _sb(144, BF), "oh": _sb(128, BF), "mr": _sb(128, BF), "cum": _sb(128, BF),
-    "js": _sb(1024, BF), "jv": _sb(1024, BF), "l1": _sb(8, F32), "lx1": _sb(32, F32), "lt1": _sb(32, F32), "mn1": _sb(16, F32),
+    "js": _sb(1280, BF), "jv": _sb(1024, BF), "l1": _sb(8, F32), "lx1": _sb(32, F32), "lt1": _sb(32, F32), "mn1": _sb(16, F32),
     "off1": _sb(16, U16), "nlp": _sb(32, BF), "nlt": _sb(32, BF),
-    "nrow": _sb(256, BF), "num": _sb(256, BF), "numt": _sb(256, BF), "tv": _sb(512, BF), "inv": _sb(256, BF),
-    "wn": _sb(272, F32), "vca": _sb(16, F32), "col": _sb(32, F32), "ec": _sb(32, F32), "cc": _sb(512, F32), "lt": _sb(512, BF),
+    "nrow": _sb(256, BF), "num": _sb(256, BF), "tv": _sb(512, BF), "inv": _sb(256, BF), "b2v": _sb(256, BF),
+    "wn": _sb(272, F32), "col": _sb(32, F32), "cc": _sb(512, F32), "lt": _sb(512, BF),
     "rr": _sb(16, F32), "tvv": _sb(64, BF), "tvt": _sb(64, BF), "rowv": _sb(256, BF), "m2": _sb(256, BF), "cum2": _sb(256, BF),
-    "l2": _sb(8, F32), "lx2": _sb(32, F32), "lt2": _sb(32, F32), "mna": _sb(16, F32), "mn2": _sb(8, F32),
-    "off2": _sb(16, U16), "offw": _sb(8, U16), "wg": _sb(128, F32),
+    "l2": _sb(8, F32), "l2v": _sb(1, F32), "lx2": _sb(32, F32), "lt2": _sb(32, F32), "mn2": _sb(16, F32),
+    "off2": _sb(16, U16), "offw": _sb(16, U16), "wg": _sb(256, F32), "wgp": _sb(128, F32),
     "ys": _sb(128, F32),
     "pw": ("psum", [128, 2048], F32), "pe": ("psum", [128, 1536], F32), "pz": ("psum", [128, 512], F32),
 }
@@ -58,23 +58,29 @@ def plan(src, cores, topo):
     can.sort(key=lambda c: (topo.die(c) == topo.die(src), c))
     half = len(cores) // 2
     helpers = {can[h]: (h, [d for d in cross if cores.index(d) // half == h]) for h in range(2)}
-    p = {"direct": direct, "helpers": helpers, "eng": {}}
+    eng = {}
     off = topo.engines(src, direct[0])
-    two = split(off, 4)
-    four = split(off, 2)
+    two, four = split(off, 4), split(off, 2)
     for i, d in enumerate(direct):
-        p["eng"]["c", d] = two[i]
-        p["eng"]["s", d] = two[3] if i == 0 else four[i - 1]
-        p["eng"]["n", d] = off[i:i + 1]
+        eng["c1", d] = eng["c2", d] = two[i]
+        eng["s1", d] = eng["s2", d] = two[3] if i == 0 else four[i - 1]
+        eng["n1", d] = eng["n2", d] = off[i:i + 1]
     for h in helpers:
+        k, serve = helpers[h]
         on = topo.engines(src, h)
-        p["eng"]["c", h] = p["eng"]["s", h] = split(on, 2)[helpers[h][0]]
-        p["eng"]["n", h] = [e for e in on if e not in off][helpers[h][0]:][:1]
-        for i, d in enumerate(helpers[h][1]):
-            e = split(topo.engines(h, d), len(helpers[h][1]))[i]
-            p["eng"]["c", h, d] = p["eng"]["s", h, d] = e
-            p["eng"]["n", h, d] = e[:1]
-    return p
+        up = [e for e in on if e not in off]
+        eng["c1", h] = split(up, 2)[k]
+        eng["s1", h] = split(off, 2)[k]
+        eng["c2", h] = split(on, 2)[k]
+        eng["s2", h] = split(up, 2)[k]
+        eng["n1", h] = eng["n2", h] = up[k:k + 1]
+        for i, d in enumerate(serve):
+            out = topo.engines(h, d)
+            quarter = split(out, 2 * len(serve))
+            eng["c1", h, d], eng["s1", h, d] = quarter[i], quarter[len(serve) + i]
+            eng["c2", h, d] = eng["s2", h, d] = split(out, len(serve))[i]
+            eng["n1", h, d] = eng["n2", h, d] = quarter[len(serve) + i][:1]
+    return {"direct": direct, "helpers": helpers, "eng": eng}
 
 
 def bits(engines):
@@ -113,24 +119,24 @@ def helper_program(g, core, T, topo):
     half, serve = p["helpers"][core]
     s, sent = T.rank_of(src), 0
 
-    def columns(t, b, w=32):
-        return t[:, w * b:w * b + w]
+    def columns(t, b):
+        return t[:, 32 * b:32 * b + 32]
 
-    for kind, n in (("c", 1), ("n", 1), ("s", 1), ("c", 2), ("s", 2), ("n", 2)):
-        g.wait_ge(T.sem["r%s%d" % (kind, n)], len(p["eng"][kind, core]))
+    for kind in ("c1", "n1", "s1", "c2", "s2", "n2"):
+        g.wait_ge(T.sem["r" + kind], len(p["eng"][kind, core]))
         tr = []
         for d in serve:
             k = T.rank_of(d) % 4
-            if n == 2 and s == 0 and T.rank_of(d) == 1:
+            if kind[1] == "2" and s == 0 and T.rank_of(d) == 1:
                 k = 0
-            if kind == "n":
-                a, b = (T.rl1[:], T.lnd[s]) if n == 1 else (T.rl2[:], T.lwd[s])
-            elif kind == "s":
-                a, b = (columns(T.r1s, k), columns(T.xhs, s)) if n == 1 else (columns(T.r2s, k), columns(T.l2s, s))
+            if kind[0] == "n":
+                a, b = (T.rl1[:], T.lnd[s]) if kind == "n1" else (T.rl2[:], T.lwd[s])
+            elif kind[0] == "s":
+                a, b = (columns(T.r1s, k), columns(T.xhs, s)) if kind == "s1" else (columns(T.r2s, k), columns(T.l2s, s))
             else:
-                a, b = (columns(T.r1c, k), columns(T.xh, s)) if n == 1 else (columns(T.r2c, k), columns(T.l2c, s))
+                a, b = (columns(T.r1c, k), columns(T.xh, s)) if kind == "c1" else (columns(T.r2c, k), columns(T.l2c, s))
                 a, b = a.bitcast(dt.uint8), b.bitcast(dt.uint8)
-            tr.append(transfer(core, d, p["eng"][kind, core, d], T.sem["%s%d" % (kind, n)], a, b, topo))
+            tr.append(transfer(core, d, p["eng"][kind, core, d], T.sem[kind], a, b, topo))
             sent += len(p["eng"][kind, core, d])
         g.remote_dma_fused(tr, local_sem=T.sem.sent)
     g.wait_ge(T.sem.sent, sent)
@@ -236,10 +242,11 @@ def rank_program(g, core, T, topo):
     place = {b: (b if me or b != 1 else 0) for b in range(NR)}
 
     k_p2 = done("p", g.iota(T.p2[:], [[0, 2]], 0, 1))
-    k_d0r = iota(T.d0r[:], [[0, 16], [1, 8]], 0, 0)
-    k_vr = iota(T.vr[:], [[1, 8]], 0, 0)
     k_xa = iota(T.xa[:], [[0, 2], [1, 2], [0, 8]], 0, 0)
     k_xb = iota(T.xb[:], [[0, 4], [1, 8]], 0, 0)
+    k_vr = iota(T.vr[:], [[1, 8]], 0, 0)
+    k_d0r = iota(T.d0r[:], [[0, 16], [1, 8]], 0, 0)
+    k_zt = fill(T.zt[:], 0.0)
     k_ones = fill(T.ones[:], 1.0)
     k_zb = fill(T.zb[:], 0.0)
     k_nlp = fill(T.nlp[:, 16:32], 0.0)
@@ -251,7 +258,7 @@ def rank_program(g, core, T, topo):
             return done("v", g.vector.tensor_scalar(d, T.p2[:], shift, mask, A.arith_shift_right, A.bitwise_and))
         return done("v", g.vector.tensor_scalar(d, T.p2[:], mask, None, A.bitwise_and))
 
-    cf = {n: T.cf[:, i:i + 1] for i, n in enumerate(("a7", "u", "uh", "ul", "blk", "q", "t", "t1", "fx", "t2", "bk4", "b2"))}
+    cf = {n: T.cf[:, i:i + 1] for i, n in enumerate(("a7", "u", "uh", "ul", "q", "t", "t1", "fx", "t2", "b2", "p0", "h", "hq", "hq2"))}
     ka, kuh, kul = bitsof(0, 0, 7), bitsof(2, 4, 1), bitsof(3, 3, 1)
     k_of1 = copy(T.of1[:], T.ia[:, 0:2], ka)
     c_a7 = copy(cf["a7"], T.ia[:, 0:1], ka)
@@ -259,22 +266,21 @@ def rank_program(g, core, T, topo):
     c_ul = copy(cf["ul"], T.ia[:, 6:7], kul)
     c_fx = ts(cf["fx"], cf["a7"], 0.0, A.is_equal, None, None, c_a7)
     c_t = ts(cf["t"], cf["ul"], 16.0, A.mult, 0.5, A.add, c_ul)
-    k_d0 = ts(T.d0[:], T.d0r[:], 0.0, A.is_equal, -BIG, A.mult, k_d0r)
-    c_t1 = ts(cf["t1"], cf["uh"], 8.0, A.mult, cf["t"], A.add, c_t)
-    k_fix = ts(T.fix[:], T.ones[:], cf["fx"], A.mult, None, None, k_ones, c_fx)
     k_mk1a = ts(T.mk1a[:], T.xa[:], cf["uh"], A.not_equal, 2000.0, A.mult, k_xa, c_uh)
     k_mk1b = ts(T.mk1b[:], T.xb[:], NS1 - 0.5, A.is_lt, 128.0, A.mult, k_xb)
+    c_t1 = ts(cf["t1"], cf["uh"], 8.0, A.mult, cf["t"], A.add, c_t)
+    k_fix = ts(T.fix[:], T.ones[:], cf["fx"], A.mult, None, None, k_ones, c_fx)
     k_th1 = ts(T.th1[:], T.vr[:], cf["t1"], A.add, None, None, k_vr, c_t1)
-    k_mk1 = tt(T.mk1[:], T.mk1a[:], T.mk1b[:], A.add, k_mk1b)
+    k_d0 = ts(T.d0[:], T.d0r[:], 0.0, A.is_equal, -BIG, A.mult, k_d0r)
 
     t = ld_r
     for w in (32, 64, 128, 256):
         t = copy(T.rte[:, w:2 * w], T.rte[:, 0:w], t)
     q_r = quant(T.rq[:], T.rs[:], T.rte[:], t)
-    k_zt = fill(T.zt[:], 0.0)
     q_x = quant(T.xq[:, 0:128], T.xs[:, 0:128], T.xt[:], ld_x)
     m_g = mm(T.pw[:, 0:128], T.rq[:], T.rs[:], T.xq[:, 0:128], T.xs[:, 0:128], True, True, q_x)
     k_zero1 = quant(T.xq[:, 128:256], T.xs[:, 128:256], T.zt[:], k_zt)
+    k_mk1 = tt(T.mk1[:], T.mk1a[:], T.mk1b[:], A.add, k_mk1b)
     v_t1 = turn(T.t1[:], T.pw[:, 0:128], m_g)
     v_rm = scan(T.rm[:], T.d0[:], T.t1[:], 0.0, A.add, A.max, v_t1, k_d0)
     for k in range(4):
@@ -308,13 +314,12 @@ def rank_program(g, core, T, topo):
     p = plan(core, T.cores, topo)
     sent = [0]
 
-    def send(kind, stage, tos, src_of, dst_of, *deps):
+    def send(kind, tos, src_of, dst_of, *deps):
         wait("p", deps)
         tr = []
         for to in tos:
             e = p["eng"][kind, to]
-            name = kind + stage if to in p["direct"] else "r" + kind + stage
-            tr.append(transfer(core, to, e, T.sem[name], src_of(to), dst_of(to), topo))
+            tr.append(transfer(core, to, e, T.sem[kind if to in p["direct"] else "r" + kind], src_of(to), dst_of(to), topo))
             sent[0] += len(e)
         g.remote_dma_fused(tr, local_sem=T.sem.sent)
 
@@ -342,43 +347,40 @@ def rank_program(g, core, T, topo):
             return land_n if to in p["direct"] else relay_n
 
         hs, ds = sorted(p["helpers"]), p["direct"]
-        send("c", stage, hs, c_src, c_dst, dep_c)
-        send("s", stage, hs, s_src, s_dst, dep_s)
-        send("c", stage, ds, c_src, c_dst)
+        send("c" + stage, hs, c_src, c_dst, dep_c)
+        send("s" + stage, hs, s_src, s_dst, dep_s)
+        send("c" + stage, ds, c_src, c_dst)
         if stage == "1":
-            send("n", stage, hs + ds, lambda to: numbers, n_dst, dep_n)
-        send("s", stage, ds[:1], s_src, s_dst)
-        send("s", stage, ds[1:], s_src, s_dst)
+            send("n" + stage, hs + ds, lambda to: numbers, n_dst, dep_n)
+        send("s" + stage, ds[:1], s_src, s_dst)
+        send("s" + stage, ds[1:], s_src, s_dst)
         if stage == "2":
-            send("n", stage, hs + ds, lambda to: numbers, n_dst, dep_n)
+            send("n" + stage, hs + ds, lambda to: numbers, n_dst, dep_n)
 
     send_stage("1", T.s1c, T.s1s, T.xh, T.xhs, T.r1c, T.r1s, {b: b for b in range(NR)}, v_s1, a_s1, T.nld[:], T.lnd[me], T.rl1[:], d_nl)
 
-    k_xc = iota(T.xc[:], [[0, 2], [1, 4], [0, 4]], 0, 0)
-    k_xd = iota(T.xd[:], [[0, 8], [1, 4]], 0, 0)
-    k_s128 = iota(T.s128[:], [[128, 8], [0, 32]], 0, 0)
-    k_oh32 = iota(T.oh32[:], [[32, 8]], 16, 0)
-    wait("p", [k_ones])
-    k_tri = done("p", g.affine_select(T.tri[:], T.ones[:], [[-1, 128]], A.is_gt, 0.0, 0, 1))
     q_w = quant(T.wq[:], T.ws[:], T.wt[:], ld_w)
+    k_127 = fill(T.c127[:], 127.5)
+    k_s128 = iota(T.s128[:], [[128, 8], [0, 32]], 0, 0)
+    k_oh32 = iota(T.oh32[:], [[32, 8]], 0, 0)
+    wait("p", [k_127])
+    k_tri = done("p", g.affine_select(T.tri[:], T.c127[:], [[-1, 128]], A.is_gt, -1.0, 0, 1))
     z2 = quant(T.xh[:, 256:384], T.xhs[:, 256:384], T.zt[:])
     z3 = quant(T.xh[:, 640:768], T.xhs[:, 640:768], T.zt[:])
     k_tv0 = fill(T.tv[:, 128:256], 0.0)
-    ku, kblk, kq, k3 = bitsof(1, 3, 3), bitsof(4, 5, 3), bitsof(5, 0, 15), bitsof(6, 0, 3)
+    ku, kq, k0, k1, k2 = bitsof(1, 3, 3), bitsof(4, 0, 15), bitsof(5, 0, 1), bitsof(6, 1, 1), bitsof(7, 2, 1)
     c_u = copy(cf["u"], T.ia[:, 2:3], ku)
-    c_blk = copy(cf["blk"], T.ia[:, 8:9], kblk)
-    c_q = copy(cf["q"], T.ia[:, 10:11], kq)
-    k_of2 = copy(T.of2[:], T.ia[:, 12:14], k3)
-    k_b2 = ts(cf["b2"], cf["a7"], 2.0, A.mult, None, None)
+    c_q = copy(cf["q"], T.ia[:, 8:9], kq)
+    c_p0 = copy(cf["p0"], T.ia[:, 10:11], k0)
+    c_h = ts(cf["h"], T.ia[:, 12:13], float(XH_H), A.mult, 128.0, A.add, k1)
+    k_b2 = ts(cf["b2"], cf["a7"], 2.0, A.mult, 8.0, A.add)
+    k_of2 = ts(T.of2[:], T.ia[:, 14:16], 2.0, A.mult, cf["p0"], A.add, k2, c_p0)
     c_t2 = ts(cf["t2"], cf["u"], 4.0, A.mult, 0.5, A.add, c_u)
-    c_bk4 = ts(cf["bk4"], cf["blk"], 4.0, A.add, None, None, c_blk)
-    k_bm0 = ts(T.bm[:, 0:8], T.vr[:], cf["blk"], A.is_equal, None, None)
-    k_mk2b = ts(T.mk2b[:], T.xd[:], NS2 - 0.5, A.is_lt, 256.0, A.mult, k_xd)
-    k_mk2a = ts(T.mk2a[:], T.xc[:], cf["u"], A.not_equal, 2000.0, A.mult, k_xc)
-    k_bm1 = ts(T.bm[:, 8:16], T.vr[:], cf["bk4"], A.is_equal, None, None, c_bk4)
+    c_hq = ts(cf["hq"], cf["q"], 2.0, A.mult, 2.0, A.add, c_q)
+    k_mk2 = ts(T.mk2[:], T.xa[:], cf["ul"], A.not_equal, 2000.0, A.mult)
     k_th2 = ts(T.th2[:], T.vr[:, 0:4], cf["t2"], A.add, None, None, c_t2)
-    k_mk2 = tt(T.mk2[:], T.mk2a[:], T.mk2b[:], A.add, k_mk2a)
-    k_ofh = ts(T.ofh[:], T.oh32[:], cf["q"], A.add, None, None, k_oh32, c_q)
+    c_hq2 = tt(cf["hq2"], cf["hq"], cf["p0"], A.subtract, c_hq)
+    k_ofh = ts(T.ofh[:], T.oh32[:], cf["hq2"], A.add, None, None, k_oh32, c_hq2)
     f_m = fill(T.r2m[:, 64:512], 0.0)
     f_m2 = fill(T.r2m[:, 36:64], 0.0, ld_2)
     q_m = quant(T.mq[:], T.ms[:], T.r2m[:], f_m2)
@@ -397,16 +399,20 @@ def rank_program(g, core, T, topo):
           dma("y", T.l2c[:, 256:272].bitcast(dt.uint8), T.xh[:, 256:272].bitcast(dt.uint8)),
           dma("y", T.l2s[:, 256:272], T.xhs[:, 256:272])]
 
-    n_c, n_s, n_n = (arrivals(k, core, T.cores, topo) for k in "csn")
-    d_nr = dma("y", T.nrow[0:1, 0:256], T.lnd[:, 16 * me:16 * me + 16, :], ("n1", n_n), d_own)
+    n_in = {k: arrivals(k, core, T.cores, topo) for k in ("c1", "s1", "n1", "c2", "s2", "n2")}
+    d_nr = dma("y", T.nrow[0:1, 0:256], T.lnd[:, 16 * me:16 * me + 16, :], ("n1", n_in["n1"]), d_own)
     wait("p", [d_nr])
     g_num = done("p", g.partition_broadcast(T.num[:], T.nrow[0:1, 0:256], 128))
-    ready = [("c1", n_c), ("s1", n_s), v_own, a_own]
+    ready = [("c1", n_in["c1"]), ("s1", n_in["s1"]), v_own, a_own]
     mw = []
     for i in range(4):
         mw.append(mm(T.pw[:, 512 * i:512 * i + 256], T.wq[:, 128 * i:128 * i + 128], T.ws[:, 128 * i:128 * i + 128],
                      T.xh[:, 0:256], T.xhs[:, 0:256], True, True, q_w, ready, v_t1))
-    col = {n: T.col[:, 2 * i:2 * i + 2] for i, n in enumerate(("num", "inv", "n2", "fe", "sc", "corr", "cc", "A", "F", "F2", "FI", "D", "nI"))}
+    col = {n: T.col[:, 2 * i:2 * i + 2] for i, n in enumerate(("e8", "n2", "fe", "sc", "corr", "cc", "A", "F", "F2", "nI"))}
+
+    def one(n, h):
+        return col[n][:, h:h + 1]
+
     rel = []
     for i in range(4):
         o, ps = T.ht[:, i:1024:4], T.pw[:, 512 * i:512 * i + 256]
@@ -415,96 +421,92 @@ def rank_program(g, core, T, topo):
         else:
             rel.append(act(o, ps, AF.Relu, mw[i], scale=0.0625))
     q_h = quant(T.xh[:, XH_H:XH_H + 256], T.xhs[:, XH_H:XH_H + 256], T.ht[:], rel)
-    a_va = act(T.inv[:], T.num[:], AF.Sign, g_num, scale=-1.0, bias=127.5, accum_out=T.col[:, 24:25])
-    a_vb = act(T.tv[:, 256:384], T.num[:, 0:128], AF.Sign, scale=-1.0, bias=127.5)
-    v_nt = turn(T.numt[:], T.num[:], g_num)
-    v_ta = tt(T.tv[:, 0:128], T.tri[:], T.inv[:, 0:128], A.mult, a_va, k_tri)
-    v_tb = tt(T.tv[:, 384:512], T.tri[:], T.inv[:, 128:256], A.mult)
-    v_ca = tt(T.vca[:, 0:8], T.numt[:, 0:256:32], T.bm[:, 0:8], A.mult, v_nt, k_bm1)
-    v_cb = tt(T.vca[:, 8:16], T.numt[:, 0:256:32], T.bm[:, 8:16], A.mult)
-    v_ni = ts(T.col[:, 25:26], T.col[:, 24:25], -0.5, A.mult, 128.0, A.add)
-    v_na2 = total(T.col[:, 0:1], T.vca[:, 0:8], v_ca)
-    v_nb2 = total(T.col[:, 1:2], T.vca[:, 8:16], v_cb)
-    v_i16 = ts(col["inv"], col["num"], 127.5, A.is_gt, 32.0, A.mult, v_nb2)
     for h in range(2):
         a = XH_H + 128 * h
         m_e = mm(T.pe[:, 512 * h:512 * h + 128], T.xh[:, a:a + 128], T.xhs[:, a:a + 128], T.mq[:], T.ms[:], True, True, q_h, q_m)
     m_row = mm(T.pe[:, 1024:1280], T.eq[:], T.es[:], T.xh[:, XH_H:XH_H + 256], T.xhs[:, XH_H:XH_H + 256], True, True, q_e)
-    v_e0 = copy(T.ec[:, 0:16], T.pe[:, 0:16], m_e)
-    v_e1 = copy(T.ec[:, 16:32], T.pe[:, 512:528])
-    e8 = T.ec[:, 8:32:16]
+    v_ta = tt(T.tv[:, 0:128], T.num[:, 0:128], T.tri[:], A.is_lt, g_num, k_tri)
+    v_tb = tt(T.tv[:, 384:512], T.num[:, 128:256], T.tri[:], A.is_lt)
+    v_tc = ts(T.tv[:, 256:384], T.num[:, 0:128], 127.5, A.is_lt, None, None)
+    a_va = act(T.inv[:], T.num[:], AF.Sign, g_num, scale=-1.0, bias=127.5, accum_out=one("nI", 0))
+    key = T.pe[:, 8:1024:512]
     f = 0.6 * 2.0 ** -23
-    v_n2 = ts(col["n2"], e8, -f, A.mult, 1e-30, A.max, v_e1)
-    v_fe = ts(col["fe"], e8, f, A.mult, None, None)
-    v_sc = tt(col["sc"], col["fe"], col["n2"], A.max, v_fe)
+    v_fe = ts(col["fe"], key, f, A.mult, None, None, m_e)
+    v_n2 = ts(col["n2"], key, -f, A.mult, 1e-30, A.max)
+    v_e8 = copy(col["e8"], key)
+    v_sc = tt(col["sc"], col["fe"], col["n2"], A.max, v_n2)
     ac = []
     for h in range(2):
-        ac.append(act(T.cc[:, 256 * h:256 * h + 256], T.tv[:, 256 * h:256 * h + 256], AF.Identity, v_sc, v_tb, a_vb, k_tv0,
-                      scale=T.col[:, 8 + h:9 + h], bias=T.ec[:, 8 + 16 * h:9 + 16 * h]))
+        ac.append(act(T.cc[:, 256 * h:256 * h + 256], T.tv[:, 256 * h:256 * h + 256], AF.Identity, v_sc, v_tc, k_tv0,
+                      scale=one("sc", h), bias=one("e8", h)))
+    v_ni = ts(one("nI", 1), one("nI", 0), -0.5, A.mult, 128.0, A.add, a_va)
     for h in range(2):
-        v_r = scan(T.rr[:, 8 * h:8 * h + 8], T.d0[:, 0:8], T.ec[:, 16 * h:16 * h + 8], 0.0, A.add, A.max)
-    v_co = ts(col["corr"], e8, 0.0, A.is_gt, T.col[:, 25:26], A.mult, v_ni)
+        v_r = scan(T.rr[:, 8 * h:8 * h + 8], T.d0[:, 0:8], T.pe[:, 512 * h:512 * h + 8], 0.0, A.add, A.max)
+    v_co = ts(col["corr"], col["e8"], 0.0, A.is_gt, one("nI", 1), A.mult, v_ni)
     v_cc = ts(col["cc"], col["corr"], DF - 0.5, A.add, None, None, v_co)
     for h in range(2):
-        a_f = act(T.js[:, 512 + 8 * h:520 + 8 * h], T.rr[:, 8 * h:8 * h + 8], AF.Sign, v_r, scale=-1.0, bias=T.rr[:, 8 * h + 7:8 * h + 8], accum_out=T.col[:, 16 + h:17 + h])
+        a_f = act(T.js[:, 768 + 8 * h:776 + 8 * h], T.rr[:, 8 * h:8 * h + 8], AF.Sign, v_r, scale=-1.0, bias=T.rr[:, 8 * h + 7:8 * h + 8], accum_out=one("F", h))
     vl = []
     for h in range(2):
         vl.append(tt(T.lt[:, 256 * h:256 * h + 256], T.pe[:, 1024:1280], T.cc[:, 256 * h:256 * h + 256], A.is_lt, ac[h], m_row))
-    a_a = act(T.js[:, 768:1024], T.lt[:, 0:256], AF.Copy, vl[0], accum_out=T.col[:, 14:15])
-    v_f2 = ts(col["F2"], col["F"], 2.0, A.mult, None, None, a_f)
-    v_a1 = total(T.col[:, 15:16], T.lt[:, 256:512], vl[1])
-    v_fi = tt(col["FI"], col["F2"], col["inv"], A.add, v_f2, v_i16)
-    v_d = tt(col["D"], col["A"], col["cc"], A.is_gt, v_a1, a_a, v_cc)
-    v_v = tt(T.tvv[:, 0:64:32], col["FI"], col["D"], A.add, v_d, v_fi, k_tvv)
-    v_tv = turn(T.tvt[:], T.tvv[:], v_v)
+    a_a = act(T.js[:, 1024:1280], T.lt[:, 0:256], AF.Copy, vl[0], accum_out=one("A", 0))
+    v_f2 = ts(col["F2"], col["F"], 2.0, A.mult, 8.0, A.add, a_f)
+    v_a1 = total(one("A", 1), T.lt[:, 256:512], vl[1])
+    v_v0 = ts(T.tvv[:, 0:1], one("A", 0), one("cc", 0), A.is_gt, one("F2", 0), A.add, a_a, v_cc, v_f2, k_tvv)
+    v_v1 = ts(T.tvv[:, 32:33], one("A", 1), one("cc", 1), A.is_gt, one("F2", 1), A.add, v_a1)
+    v_tv = turn(T.tvt[:], T.tvv[:], v_v0, v_v1)
     wait("p", [v_tv])
     b = [done("p", g.partition_broadcast(T.rowv[:, 64 * q:64 * q + 64], T.tvt[32 * q:32 * q + 1, 0:64], 128)) for q in range(4)]
-    v_wn = tt(T.wn[:, 0:256], T.num[:], T.s128[:], A.add, k_s128)
+    v_b2 = ts(T.b2v[:], T.num[:], 127.5, A.is_lt, cf["b2"], A.mult, k_b2)
     for q in range(4):
         for h in range(2):
-            v_m2 = ts(T.m2[:, 128 * h + 32 * q:128 * h + 32 * q + 32], T.rowv[:, 64 * q + 32 * h:64 * q + 32 * h + 32], cf["b2"], A.is_equal, None, None, b[q], k_b2)
+            k = 128 * h + 32 * q
+            v_m2 = tt(T.m2[:, k:k + 32], T.rowv[:, 64 * q + 32 * h:64 * q + 32 * h + 32], T.b2v[:, k:k + 32], A.is_equal, b[q], v_b2)
     v_c2 = scan(T.cum2[:], T.zrow[:], T.m2[:], 0.0, A.add, A.add, v_m2, k_zrow)
     acc = []
     for v in range(NS2):
         acc.append(act(T.js[:, 256 * v:256 * v + 256], T.cum2[:], AF.Sign, v_c2, k_th2, scale=-1.0, bias=T.th2[:, v:v + 1], accum_out=T.l2[:, v:v + 1]))
-    for v in range(NS2, 4):
-        part[v] = ts(T.jv[:, 256 * v:256 * v + 256], T.cum2[:], T.th2[:, v:v + 1], A.is_le, 2.0, A.mult, v_c2, v_lx)
-    for v in range(NS2, 4):
-        acc.append(total(T.l2[:, v:v + 1], T.jv[:, 256 * v:256 * v + 256], part[v]))
-    v_lx = tt(T.lx2[:], T.l2[:, 0:8].indirect(T.of2[:, 0:2]), T.mk2[:], A.add, acc, k_mk2, k_of2, k_l2)
+    v_p = ts(T.jv[:, 0:256], T.cum2[:], T.th2[:, NS2:NS2 + 1], A.is_le, 2.0, A.mult, v_c2, v_lx)
+    v_p = total(T.l2v[:], T.jv[:, 0:256], v_p)
+    v_p = ts(T.l2[:, NS2:NS2 + 1], T.l2v[:], -256.0, A.add, None, None, v_p)
+    v_lx = tt(T.lx2[:], T.l2[:, 0:8].indirect(T.of2[:, 0:2]), T.mk2[:], A.add, acc, v_p, k_mk2, k_of2, k_l2)
     v_lt = turn(T.lt2[:], T.lx2[:], v_lx)
-    v_ma = tt(T.mna[:], T.lt2[:, 0:16], T.lt2[:, 16:32], A.min, v_lt)
-    v_mn = tt(T.mn2[:], T.mna[:, 0:8], T.mna[:, 8:16], A.min, v_ma)
-    v_o0 = ts(T.off2[:, 0:16:2], T.mn2[:], 0.5, A.mult, None, None, v_mn)
-    v_o1 = ts(T.off2[:, 1:16:2], T.mn2[:], 0.5, A.mult, float(XH_H), A.add, v_mn)
-    v_s2 = copy(T.s2c[:].bitcast(dt.uint32), T.xh[:].bitcast(dt.uint32).indirect(T.off2[:]), v_o0, v_o1, ready, q_h, z2, z3)
+    v_m0 = tt(T.mn2[:, 0:8], T.lt2[:, 0:8], T.lt2[:, 8:16], A.min, v_lt)
+    v_m1 = tt(T.mn2[:, 8:16], T.lt2[:, 16:24], T.lt2[:, 24:32], A.min)
+    v_o0 = ts(T.off2[:, 0:16:2], T.mn2[:, 0:8], 0.5, A.mult, cf["h"], A.add, v_m0, c_h)
+    v_o1 = ts(T.off2[:, 1:16:2], T.mn2[:, 8:16], 0.5, A.mult, cf["h"], A.add, v_m1)
+    v_s2 = copy(T.s2c[:].bitcast(dt.uint32), T.xh[:].bitcast(dt.uint32).indirect(T.off2[:]), v_o1, ready, q_h, z2, z3)
     a_s2 = act(T.s2s[:], T.xhs[:].indirect(T.off2[:]), AF.Copy, v_o1, ready)
-    v_ow = ts(T.offw[:], T.mn2[:], 0.5, A.mult, None, None)
-    v_wg = copy(T.wg[:], T.wn[:].indirect(T.offw[:]), v_ow, v_wn, k_wn)
+    v_w0 = ts(T.offw[:, 0:16:2], T.mn2[:, 0:8], 0.5, A.mult, 128.0, A.add)
+    v_w1 = ts(T.offw[:, 1:16:2], T.mn2[:, 8:16], 0.5, A.mult, 128.0, A.add)
+    v_wn = tt(T.wn[:, 0:256], T.num[:], T.s128[:], A.add, k_s128)
+    v_wg = copy(T.wg[:], T.wn[:].indirect(T.offw[:]), v_wn, v_w1, k_wn)
+    v_g0 = copy(T.wgp[:, 0:128:2], T.wg[:, 0:256:4], v_wg)
+    v_g1 = copy(T.wgp[:, 1:128:2], T.wg[:, 1:256:4])
     runs = [(0, 0, 128)] if me else [(0, 16, 16), (16, 0, 16), (32, 32, 96)]
     d_wg, d_wo = [], []
     for to, fr, n in runs:
-        d_wg.append(dma("y", T.wgd[to:to + n, 0], T.wg[0:1, fr:fr + n], v_wg))
-        d_wo.append(dma("s", T.lwd[me, to:to + n, 0], T.wg[0:1, fr:fr + n], v_wg))
+        d_wg.append(dma("y", T.wgd[to:to + n, 0], T.wgp[0:1, fr:fr + n], v_g1))
+        d_wo.append(dma("s", T.lwd[me, to:to + n, 0], T.wgp[0:1, fr:fr + n], v_g1))
     send_stage("2", T.s2c, T.s2s, T.l2c, T.l2s, T.r2c, T.r2s, place, v_s2, a_s2, T.wgd[:], T.lwd[me], T.rl2[:], d_wg)
 
-    ready = [("c2", n_c), ("s2", n_s), dz]
+    ready = [("c2", n_in["c2"]), ("s2", n_in["s2"]), dz]
     out = (T.pz[:, 0:128], T.pw[:, 512:640])
     my = []
     for k in range(2):
         a = 128 * k
         mm(out[k], T.vxq[:], T.vxs[:], T.l2c[:, a:a + 128], T.l2s[:, a:a + 128], True, False, ready, q_vx, q_vh, rel)
-        my.append(mm(out[k], T.vhq[:], T.vhs[:], T.l2c[:, a + 16:a + 144], T.l2s[:, a + 16:a + 144], False, True))
-    v_hp = copy(T.hp[:].bitcast(dt.uint32), T.l2c[:, 0:256].bitcast(dt.uint32).indirect(T.ofh[:]), ready, k_ofh)
+        my.append(mm(out[k], T.vhq[:], T.vhs[:], T.l2c[:, a + 2:a + 130], T.l2s[:, a + 2:a + 130], False, True))
     a_hp = act(T.hps[:], T.l2s[:, 0:256].indirect(T.ofh[:]), AF.Copy, ready, k_ofh)
+    v_hp = copy(T.hp[:].bitcast(dt.uint32), T.l2c[:, 0:256].bitcast(dt.uint32).indirect(T.ofh[:]), ready, k_ofh)
+    for r in range(2):
+        v_y = copy(T.ys[:, r:64:2], T.pz[:, r:128:4], my[0])
+        a_y = act(T.ys[:, 64 + r:128:2], T.pw[:, 512 + r:640:4], AF.Copy, my[1])
     dma("y", T.oc[:, 0:512], T.hp[:].bitcast(dt.uint8), v_hp)
-    for i in range(4):
-        v_y = copy(T.ys[:, 16 * i:16 * i + 16], T.pz[:, 32 * i:32 * i + 16], my[0])
-        a_y = act(T.ys[:, 64 + 16 * i:80 + 16 * i], T.pw[:, 512 + 32 * i:528 + 32 * i], AF.Copy, my[1])
-    dma("s", T.y[:, 64:128], T.ys[:, 64:128], a_y)
-    dma("y", T.y[:, 0:64], T.ys[:, 0:64], v_y)
     for k in range(4):
-        dma("s" if k % 2 else "y", T.osc[4 * k:4 * k + 4, 0:128], T.hps[32 * k:32 * k + 4, 0:128], a_hp)
-    dma("y", T.who[0:1, 0:128], T.lwd[:, 16 * me:16 * me + 16, 0], ("n2", n_n), d_wo)
+        dma("y", T.osc[4 * k:4 * k + 4, 0:128], T.hps[32 * k:32 * k + 4, 0:128], a_hp)
+    dma("y", T.y[:, 0:64], T.ys[:, 0:64], v_y)
+    dma("s", T.y[:, 64:128], T.ys[:, 64:128], a_y)
+    dma("s", T.who[0:1, 0:128], T.lwd[:, 16 * me:16 * me + 16, 0], ("n2", n_in["n2"]), d_wo)
     g.wait_ge(T.sem.sent, sent[0])
     wait("p", [(s, everything[s]) for s in everything])

from concourse.bass import DstId, RemoteDMATransfer
from concourse.mybir import dt, AluOpType, AxisListType, ActivationFunctionType

F8, U8, U16, BF, F32, I32 = "float8_e4m3fn_x4", "uint8", "uint16", "bfloat16", "float32", "int32"
DF, NR = 64, 8
NS1, NS2 = 5, 3
BIG = 1.0e29
XH_H = 384


def _sb(w, d):
    return ("sbuf", [128, w], d)


SCRATCH = {
    "xt": _sb(512, BF), "rte": _sb(512, BF), "wt": _sb(2048, BF), "r2m": _sb(512, BF), "r2r": _sb(512, BF),
    "vxt": _sb(512, BF), "vht": _sb(512, BF), "zt": _sb(512, BF), "ht": _sb(1024, BF),
    "xq": _sb(256, F8), "xs": _sb(256, U8), "rq": _sb(128, F8), "rs": _sb(128, U8), "wq": _sb(512, F8), "ws": _sb(512, U8),
    "mq": _sb(128, F8), "ms": _sb(128, U8), "eq": _sb(128, F8), "es": _sb(128, U8),
    "vxq": _sb(128, F8), "vxs": _sb(128, U8), "vhq": _sb(128, F8), "vhs": _sb(128, U8),
    "s1c": _sb(256, F8), "s1s": _sb(256, U8), "r1c": _sb(128, F8), "r1s": _sb(128, U8), "xh": _sb(768, F8), "xhs": _sb(768, U8),
    "s2c": _sb(256, F8), "s2s": _sb(256, U8), "r2c": _sb(128, F8), "r2s": _sb(128, U8), "l2c": _sb(272, F8), "l2s": _sb(272, U8),
    "hp": _sb(128, F8), "hps": _sb(128, U8),
    "nld": ("dram", [128, 2], BF), "rl1": ("dram", [128, 2], BF), "lnd": ("dram", [8, 128, 2], BF),
    "wgd": ("dram", [128, 1], F32), "rl2": ("dram", [128, 1], F32), "lwd": ("dram", [8, 128, 1], F32),
    "p2": _sb(2, I32), "ia": _sb(16, I32), "cf": _sb(16, F32), "of1": _sb(2, U16), "of2": _sb(2, U16), "ofh": _sb(8, U16),
    "vr": _sb(8, F32), "th1": _sb(8, F32), "th2": _sb(4, F32), "ones": _sb(128, BF), "fix": _sb(128, BF), "zrow": _sb(256, BF),
    "d0r": _sb(128, F32), "d0": _sb(128, F32), "xa": _sb(32, F32), "xb": _sb(32, F32),
    "mk1": _sb(32, F32), "mk1b": _sb(32, F32), "mk1a": _sb(32, F32), "mk2": _sb(32, F32),
    "c127": _sb(128, BF), "tri": _sb(128, BF), "s128": _sb(256, F32), "oh32": _sb(8, F32),
    "t1": _sb(128, F32), "rm": _sb(128, F32), "zb": _sb(144, BF), "oh": _sb(128, BF), "mr": _sb(128, BF), "cum": _sb(128, BF),
    "js": _sb(1280, BF), "jv": _sb(1024, BF), "l1": _sb(8, F32), "lx1": _sb(32, F32), "lt1": _sb(32, F32), "mn1": _sb(16, F32),
    "off1": _sb(16, U16), "nlp": _sb(32, BF), "nlt": _sb(32, BF),
    "nrow": _sb(256, BF), "num": _sb(256, BF), "tv": _sb(512, BF), "inv": _sb(256, BF), "b2v": _sb(256, BF),
    "wn": _sb(272, F32), "col": _sb(32, F32), "cc": _sb(512, F32), "lt": _sb(512, BF),
    "rr": _sb(16, F32), "tvv": _sb(64, BF), "tvt": _sb(64, BF), "rowv": _sb(256, BF), "m2": _sb(256, BF), "cum2": _sb(256, BF),
    "l2": _sb(8, F32), "l2v": _sb(1, F32), "lx2": _sb(32, F32), "lt2": _sb(32, F32), "mn2": _sb(16, F32),
    "off2": _sb(16, U16), "offw": _sb(16, U16), "wg": _sb(256, F32), "wgp": _sb(128, F32),
    "ys": _sb(128, F32),
    "pw": ("psum", [128, 2048], F32), "pe": ("psum", [128, 1536], F32), "pz": ("psum", [128, 512], F32),
}
NDMA = 34
SEMAPHORES = (["kv", "ks", "kt", "kp", "sent"] + [k + n for k in ("c", "s", "n", "rc", "rs", "rn") for n in "12"]
              + ["d%d" % i for i in range(NDMA)])


def split(engines, parts):
    k = 1
    while 2 * k * parts <= len(engines):
        k *= 2
    return [engines[k * i:k * i + k] for i in range(parts)]


def plan(src, cores, topo):
    direct = [d for d in cores if d != src and topo.may_write(src, d)]
    cross = [d for d in cores if d != src and not topo.may_write(src, d)]
    can = [c for c in topo.cores_of(src) if c != src and all(topo.may_write(c, d) for d in cross)]
    can.sort(key=lambda c: (topo.die(c) == topo.die(src), c))
    half = len(cores) // 2
    helpers = {can[h]: (h, [d for d in cross if cores.index(d) // half == h]) for h in range(2)}
    eng = {}
    off = topo.engines(src, direct[0])
    two, four = split(off, 4), split(off, 2)
    for i, d in enumerate(direct):
        eng["c1", d] = eng["c2", d] = two[i]
        eng["s1", d] = eng["s2", d] = two[3] if i == 0 else four[i - 1]
        eng["n1", d] = eng["n2", d] = off[i:i + 1]
    for h in helpers:
        k, serve = helpers[h]
        on = topo.engines(src, h)
        up = [e for e in on if e not in off]
        eng["c1", h] = split(up, 2)[k]
        eng["s1", h] = split(off, 2)[k]
        eng["c2", h] = split(on, 2)[k]
        eng["s2", h] = split(up, 2)[k]
        eng["n1", h] = eng["n2", h] = up[k:k + 1]
        for i, d in enumerate(serve):
            out = topo.engines(h, d)
            quarter = split(out, 2 * len(serve))
            eng["c1", h, d], eng["s1", h, d] = quarter[i], quarter[len(serve) + i]
            eng["c2", h, d] = eng["s2", h, d] = split(out, len(serve))[i]
            eng["n1", h, d] = eng["n2", h, d] = quarter[len(serve) + i][:1]
    return {"direct": direct, "helpers": helpers, "eng": eng}


def bits(engines):
    v = 0
    for e in engines:
        v |= 1 << e
    return v


def arrivals(kind, core, cores, topo):
    n = 0
    for s in cores:
        if s != core:
            p = plan(s, cores, topo)
            if core in p["direct"]:
                n += len(p["eng"][kind, core])
            for h in p["helpers"]:
                if core in p["helpers"][h][1]:
                    n += len(p["eng"][kind, h, core])
    return n


def transfer(core, to, engines, sem, src, dst, topo):
    rid, pid = topo.addr(to, core)
    return RemoteDMATransfer(dst_ids=[DstId(rid=rid, pnc=pid)], dma_engine_mask=bits(engines), remote_sem=sem, src=src, dst=dst)


def helper_program(g, core, T, topo):
    home = [c for c in T.cores if c in topo.cores_of(core)]
    if not home:
        return
    src = home[0]
    p = plan(src, T.cores, topo)
    if core not in p["helpers"]:
        return
    half, serve = p["helpers"][core]
    s, sent = T.rank_of(src), 0

    def columns(t, b):
        return t[:, 32 * b:32 * b + 32]

    for kind in ("c1", "n1", "s1", "c2", "s2", "n2"):
        g.wait_ge(T.sem["r" + kind], len(p["eng"][kind, core]))
        tr = []
        for d in serve:
            k = T.rank_of(d) % 4
            if kind[1] == "2" and s == 0 and T.rank_of(d) == 1:
                k = 0
            if kind[0] == "n":
                a, b = (T.rl1[:], T.lnd[s]) if kind == "n1" else (T.rl2[:], T.lwd[s])
            elif kind[0] == "s":
                a, b = (columns(T.r1s, k), columns(T.xhs, s)) if kind == "s1" else (columns(T.r2s, k), columns(T.l2s, s))
            else:
                a, b = (columns(T.r1c, k), columns(T.xh, s)) if kind == "c1" else (columns(T.r2c, k), columns(T.l2c, s))
                a, b = a.bitcast(dt.uint8), b.bitcast(dt.uint8)
            tr.append(transfer(core, d, p["eng"][kind, core, d], T.sem[kind], a, b, topo))
            sent += len(p["eng"][kind, core, d])
        g.remote_dma_fused(tr, local_sem=T.sem.sent)
    g.wait_ge(T.sem.sent, sent)


def rank_program(g, core, T, topo):
    me = T.rank_of(core)
    if me is None:
        helper_program(g, core, T, topo)
        return
    A, AF = AluOpType, ActivationFunctionType
    eng = {"v": g.vector, "s": g.scalar, "t": g.tensor, "p": g, "y": g.sync}
    cnt = {q: 0 for q in eng}
    seen = {q: {} for q in eng}
    ndma = [0]
    everything = {}

    def wait(q, deps):
        need, todo = {}, list(deps)
        for d in todo:
            if isinstance(d, list):
                todo.extend(d)
            else:
                need[d[0]] = max(need.get(d[0], 0), d[1])
        for sem in need:
            if seen[q].get(sem, 0) < need[sem]:
                eng[q].wait_ge(T.sem[sem], need[sem])
                seen[q][sem] = need[sem]

    def done(q, inst):
        cnt[q] += 1
        inst.then_inc(T.sem["k" + q], 1)
        everything["k" + q] = cnt[q]
        return ("k" + q, cnt[q])

    def dma(q, out, in_, *deps):
        wait(q, deps)
        sem = "d%d" % ndma[0]
        ndma[0] += 1
        eng[q].dma_start(out, in_).then_inc(T.sem[sem], 16)
        everything[sem] = 16
        return (sem, 16)

    def ts(out, in0, s1, op0, s2, op1, *deps):
        wait("v", deps)
        if op1 is None:
            return done("v", g.vector.tensor_scalar(out, in0, s1, None, op0))
        return done("v", g.vector.tensor_scalar(out, in0, s1, s2, op0, op1))

    def tt(out, a, b, op, *deps):
        wait("v", deps)
        return done("v", g.vector.tensor_tensor(out, a, b, op))

    def copy(out, in_, *deps):
        wait("v", deps)
        return done("v", g.vector.tensor_copy(out, in_))

    def fill(ap, c, *deps):
        wait("v", deps)
        return done("v", g.vector.memset(ap, c))

    def scan(out, a, b, init, op0, op1, *deps):
        wait("v", deps)
        return done("v", g.vector.tensor_tensor_scan(out, a, b, init, op0, op1))

    def turn(out, in_, *deps):
        wait("v", deps)
        return done("v", g.vector.transpose(out, in_))

    def total(out, in_, *deps):
        wait("v", deps)
        return done("v", g.vector.tensor_reduce(out, in_, AxisListType.X, A.add))

    def quant(q, s, in_, *deps):
        wait("v", deps)
        return done("v", g.vector.quantize_mx(q, s, in_))

    def act(out, in_, func, *deps, **kw):
        wait("s", deps)
        return done("s", g.scalar.activation(out, in_, func, **kw))

    def mm(out, l, ls, r, rs, start, stop, *deps):
        wait("t", deps)
        return done("t", g.tensor.matmul_mx(out, l, ls, r, rs, start, stop))

    def iota(out, pattern, base, cm):
        return done("p", g.iota(out, pattern, base, cm, allow_small_or_imprecise_dtypes=True))

    ld_x = dma("y", T.xt[:], T.x[:])
    ld_r = dma("s", T.rte[:, 0:32], T.rt[:, 0:32])
    ld_w = dma("y", T.wt[:], T.w[:], ld_x)
    ld_2 = []
    if me:
        ld_2.append(dma("y", T.r2m[:, 0:4 * me], T.r2[:, 0:4 * me]))
        ld_2.append(dma("y", T.r2m[:, 4 * me:4 * me + 4], T.r2[:, 4 * me - 4:4 * me]))
        ld_2.append(dma("y", T.r2m[:, 4 * me + 4:36], T.r2[:, 4 * me + 4:36]))
    else:
        ld_2.append(dma("y", T.r2m[:, 0:4], T.r2[:, 4:8]))
        ld_2.append(dma("y", T.r2m[:, 4:36], T.r2[:, 4:36]))
    ld_e = dma("y", T.r2r[:, 0:4], T.r2[:, 32:36])
    ld_vx = dma("y", T.vxt[:], T.vx[:])
    ld_vh = dma("y", T.vht[:], T.vh[:])
    place = {b: (b if me or b != 1 else 0) for b in range(NR)}

    k_p2 = done("p", g.iota(T.p2[:], [[0, 2]], 0, 1))
    k_xa = iota(T.xa[:], [[0, 2], [1, 2], [0, 8]], 0, 0)
    k_xb = iota(T.xb[:], [[0, 4], [1, 8]], 0, 0)
    k_vr = iota(T.vr[:], [[1, 8]], 0, 0)
    k_d0r = iota(T.d0r[:], [[0, 16], [1, 8]], 0, 0)
    k_zt = fill(T.zt[:], 0.0)
    k_ones = fill(T.ones[:], 1.0)
    k_zb = fill(T.zb[:], 0.0)
    k_nlp = fill(T.nlp[:, 16:32], 0.0)

    def bitsof(i, shift, mask):
        d = T.ia[:, 2 * i:2 * i + 2]
        wait("v", [k_p2])
        if shift:
            return done("v", g.vector.tensor_scalar(d, T.p2[:], shift, mask, A.arith_shift_right, A.bitwise_and))
        return done("v", g.vector.tensor_scalar(d, T.p2[:], mask, None, A.bitwise_and))

    cf = {n: T.cf[:, i:i + 1] for i, n in enumerate(("a7", "u", "uh", "ul", "q", "t", "t1", "fx", "t2", "b2", "p0", "h", "hq", "hq2"))}
    ka, kuh, kul = bitsof(0, 0, 7), bitsof(2, 4, 1), bitsof(3, 3, 1)
    k_of1 = copy(T.of1[:], T.ia[:, 0:2], ka)
    c_a7 = copy(cf["a7"], T.ia[:, 0:1], ka)
    c_uh = copy(cf["uh"], T.ia[:, 4:5], kuh)
    c_ul = copy(cf["ul"], T.ia[:, 6:7], kul)
    c_fx = ts(cf["fx"], cf["a7"], 0.0, A.is_equal, None, None, c_a7)
    c_t = ts(cf["t"], cf["ul"], 16.0, A.mult, 0.5, A.add, c_ul)
    k_mk1a = ts(T.mk1a[:], T.xa[:], cf["uh"], A.not_equal, 2000.0, A.mult, k_xa, c_uh)
    k_mk1b = ts(T.mk1b[:], T.xb[:], NS1 - 0.5, A.is_lt, 128.0, A.mult, k_xb)
    c_t1 = ts(cf["t1"], cf["uh"], 8.0, A.mult, cf["t"], A.add, c_t)
    k_fix = ts(T.fix[:], T.ones[:], cf["fx"], A.mult, None, None, k_ones, c_fx)
    k_th1 = ts(T.th1[:], T.vr[:], cf["t1"], A.add, None, None, k_vr, c_t1)
    k_d0 = ts(T.d0[:], T.d0r[:], 0.0, A.is_equal, -BIG, A.mult, k_d0r)

    t = ld_r
    for w in (32, 64, 128, 256):
        t = copy(T.rte[:, w:2 * w], T.rte[:, 0:w], t)
    q_r = quant(T.rq[:], T.rs[:], T.rte[:], t)
    q_x = quant(T.xq[:, 0:128], T.xs[:, 0:128], T.xt[:], ld_x)
    m_g = mm(T.pw[:, 0:128], T.rq[:], T.rs[:], T.xq[:, 0:128], T.xs[:, 0:128], True, True, q_x)
    k_zero1 = quant(T.xq[:, 128:256], T.xs[:, 128:256], T.zt[:], k_zt)
    k_mk1 = tt(T.mk1[:], T.mk1a[:], T.mk1b[:], A.add, k_mk1b)
    v_t1 = turn(T.t1[:], T.pw[:, 0:128], m_g)
    v_rm = scan(T.rm[:], T.d0[:], T.t1[:], 0.0, A.add, A.max, v_t1, k_d0)
    for k in range(4):
        v_z = ts(T.zb[:, 1 + 32 * k:33 + 32 * k], T.rm[:, 32 * k:32 * k + 32], T.rm[:, 32 * k + 7:32 * k + 8], A.is_lt, None, None, v_rm, k_zb)
    v_oh = tt(T.oh[:], T.zb[:, 0:128], T.zb[:, 1:129], A.subtract, v_z)
    v_m = turn(T.mr[:], T.oh[:], v_oh)
    v_c = scan(T.cum[:], T.fix[:], T.mr[:], 0.0, A.add, A.add, v_m, k_fix)
    acc, part = [], {}
    for v in range(NS1):
        acc.append(act(T.js[:, 128 * v:128 * v + 128], T.cum[:], AF.Sign, v_c, k_th1, scale=-1.0, bias=T.th1[:, v:v + 1], accum_out=T.l1[:, v:v + 1]))
    for v in range(NS1, 8):
        part[v] = ts(T.jv[:, 128 * v:128 * v + 128], T.cum[:], T.th1[:, v:v + 1], A.is_le, 2.0, A.mult, v_c, k_th1)
    for v in range(NS1, 8):
        acc.append(total(T.l1[:, v:v + 1], T.jv[:, 128 * v:128 * v + 128], part[v]))
    v_lx = tt(T.lx1[:], T.l1[:, 0:8].indirect(T.of1[:, 0:2]), T.mk1[:], A.add, acc, k_mk1, k_of1)
    v_lt = turn(T.lt1[:], T.lx1[:], v_lx)
    v_mn = tt(T.mn1[:], T.lt1[:, 0:16], T.lt1[:, 16:32], A.min, v_lt)
    v_o0 = ts(T.off1[:, 0:16:2], T.mn1[:, 0:8], 0.5, A.mult, None, None, v_mn)
    v_o1 = ts(T.off1[:, 1:16:2], T.mn1[:, 8:16], 0.5, A.mult, None, None, v_mn)
    v_s1 = copy(T.s1c[:].bitcast(dt.uint32), T.xq[:].bitcast(dt.uint32).indirect(T.off1[:]), v_o1, v_o0, q_x, k_zero1)
    a_n0 = act(T.nlp[:, 0:16:2], T.mn1[:, 0:8], AF.Copy, v_mn, scale=0.5)
    a_n1 = act(T.nlp[:, 1:16:2], T.mn1[:, 8:16], AF.Copy, v_mn, scale=0.5)
    a_s1 = act(T.s1s[:], T.xs[:].indirect(T.off1[:]), AF.Copy, v_o1)
    w0 = 32 * me
    a_own = act(T.xhs[:, w0:w0 + 32], T.xs[:].indirect(T.off1[:, 2 * me:2 * me + 2]), AF.Copy)
    v_nt = turn(T.nlt[:], T.nlp[:], a_n1, k_nlp)
    d_nl = dma("y", T.nld[:], T.nlt[0:16, 0:16], v_nt)
    d_own = dma("y", T.lnd[me], T.nlt[0:16, 0:16])
    v_own = copy(T.xh[:, w0:w0 + 32].bitcast(dt.uint32), T.xq[:].bitcast(dt.uint32).indirect(T.off1[:, 2 * me:2 * me + 2]))

    p = plan(core, T.cores, topo)
    sent = [0]

    def send(kind, tos, src_of, dst_of, *deps):
        wait("p", deps)
        tr = []
        for to in tos:
            e = p["eng"][kind, to]
            tr.append(transfer(core, to, e, T.sem[kind if to in p["direct"] else "r" + kind], src_of(to), dst_of(to), topo))
            sent[0] += len(e)
        g.remote_dma_fused(tr, local_sem=T.sem.sent)

    def send_stage(stage, codes, scales, land_c, land_s, relay_c, relay_s, pl, dep_c, dep_s, numbers, land_n, relay_n, dep_n):
        def part_of(t, to):
            if to in p["direct"]:
                b = pl[T.rank_of(to)]
                return t[:, 32 * b:32 * b + 32]
            h = p["helpers"][to][0]
            return t[:, 128 * h:128 * h + 128]

        def c_src(to):
            return part_of(codes, to).bitcast(dt.uint8)

        def c_dst(to):
            return (land_c[:, w0:w0 + 32] if to in p["direct"] else relay_c[:]).bitcast(dt.uint8)

        def s_src(to):
            return part_of(scales, to)

        def s_dst(to):
            return land_s[:, w0:w0 + 32] if to in p["direct"] else relay_s[:]

        def n_dst(to):
            return land_n if to in p["direct"] else relay_n

        hs, ds = sorted(p["helpers"]), p["direct"]
        send("c" + stage, hs, c_src, c_dst, dep_c)
        send("s" + stage, hs, s_src, s_dst, dep_s)
        send("c" + stage, ds, c_src, c_dst)
        if stage == "1":
            send("n" + stage, hs + ds, lambda to: numbers, n_dst, dep_n)
        send("s" + stage, ds[:1], s_src, s_dst)
        send("s" + stage, ds[1:], s_src, s_dst)
        if stage == "2":
            send("n" + stage, hs + ds, lambda to: numbers, n_dst, dep_n)

    send_stage("1", T.s1c, T.s1s, T.xh, T.xhs, T.r1c, T.r1s, {b: b for b in range(NR)}, v_s1, a_s1, T.nld[:], T.lnd[me], T.rl1[:], d_nl)

    q_w = quant(T.wq[:], T.ws[:], T.wt[:], ld_w)
    k_127 = fill(T.c127[:], 127.5)
    k_s128 = iota(T.s128[:], [[128, 8], [0, 32]], 0, 0)
    k_oh32 = iota(T.oh32[:], [[32, 8]], 0, 0)
    wait("p", [k_127])
    k_tri = done("p", g.affine_select(T.tri[:], T.c127[:], [[-1, 128]], A.is_gt, -1.0, 0, 1))
    z2 = quant(T.xh[:, 256:384], T.xhs[:, 256:384], T.zt[:])
    z3 = quant(T.xh[:, 640:768], T.xhs[:, 640:768], T.zt[:])
    k_tv0 = fill(T.tv[:, 128:256], 0.0)
    ku, kq, k0, k1, k2 = bitsof(1, 3, 3), bitsof(4, 0, 15), bitsof(5, 0, 1), bitsof(6, 1, 1), bitsof(7, 2, 1)
    c_u = copy(cf["u"], T.ia[:, 2:3], ku)
    c_q = copy(cf["q"], T.ia[:, 8:9], kq)
    c_p0 = copy(cf["p0"], T.ia[:, 10:11], k0)
    c_h = ts(cf["h"], T.ia[:, 12:13], float(XH_H), A.mult, 128.0, A.add, k1)
    k_b2 = ts(cf["b2"], cf["a7"], 2.0, A.mult, 8.0, A.add)
    k_of2 = ts(T.of2[:], T.ia[:, 14:16], 2.0, A.mult, cf["p0"], A.add, k2, c_p0)
    c_t2 = ts(cf["t2"], cf["u"], 4.0, A.mult, 0.5, A.add, c_u)
    c_hq = ts(cf["hq"], cf["q"], 2.0, A.mult, 2.0, A.add, c_q)
    k_mk2 = ts(T.mk2[:], T.xa[:], cf["ul"], A.not_equal, 2000.0, A.mult)
    k_th2 = ts(T.th2[:], T.vr[:, 0:4], cf["t2"], A.add, None, None, c_t2)
    c_hq2 = tt(cf["hq2"], cf["hq"], cf["p0"], A.subtract, c_hq)
    k_ofh = ts(T.ofh[:], T.oh32[:], cf["hq2"], A.add, None, None, k_oh32, c_hq2)
    f_m = fill(T.r2m[:, 64:512], 0.0)
    f_m2 = fill(T.r2m[:, 36:64], 0.0, ld_2)
    q_m = quant(T.mq[:], T.ms[:], T.r2m[:], f_m2)
    t = ld_e
    for w in (4, 8, 16, 32, 64, 128, 256):
        t = copy(T.r2r[:, w:2 * w], T.r2r[:, 0:w], t)
    q_e = quant(T.eq[:], T.es[:], T.r2r[:], t)
    k_zrow = fill(T.zrow[:], 0.0)
    k_tvv = fill(T.tvv[:], 0.0)
    k_wn = fill(T.wn[:, 256:272], -1.0)
    k_l2 = fill(T.l2[:, 4:8], 0.0)
    q_vx = quant(T.vxq[:], T.vxs[:], T.vxt[:], ld_vx)
    q_vh = quant(T.vhq[:], T.vhs[:], T.vht[:], ld_vh)
    dz = [dma("y", T.l2c[:, w0:w0 + 32].bitcast(dt.uint8), T.xh[:, 256:288].bitcast(dt.uint8), z2),
          dma("y", T.l2s[:, w0:w0 + 32], T.xhs[:, 256:288]),
          dma("y", T.l2c[:, 256:272].bitcast(dt.uint8), T.xh[:, 256:272].bitcast(dt.uint8)),
          dma("y", T.l2s[:, 256:272], T.xhs[:, 256:272])]

    n_in = {k: arrivals(k, core, T.cores, topo) for k in ("c1", "s1", "n1", "c2", "s2", "n2")}
    d_nr = dma("y", T.nrow[0:1, 0:256], T.lnd[:, 16 * me:16 * me + 16, :], ("n1", n_in["n1"]), d_own)
    wait("p", [d_nr])
    g_num = done("p", g.partition_broadcast(T.num[:], T.nrow[0:1, 0:256], 128))
    ready = [("c1", n_in["c1"]), ("s1", n_in["s1"]), v_own, a_own]
    mw = []
    for i in range(4):
        mw.append(mm(T.pw[:, 512 * i:512 * i + 256], T.wq[:, 128 * i:128 * i + 128], T.ws[:, 128 * i:128 * i + 128],
                     T.xh[:, 0:256], T.xhs[:, 0:256], True, True, q_w, ready, v_t1))
    col = {n: T.col[:, 2 * i:2 * i + 2] for i, n in enumerate(("e8", "n2", "fe", "sc", "corr", "cc", "A", "F", "F2", "nI"))}

    def one(n, h):
        return col[n][:, h:h + 1]

    rel = []
    for i in range(4):
        o, ps = T.ht[:, i:1024:4], T.pw[:, 512 * i:512 * i + 256]
        if i % 2 == 0:
            rel.append(ts(o, ps, 0.0, A.max, 0.0625, A.mult, mw[i]))
        else:
            rel.append(act(o, ps, AF.Relu, mw[i], scale=0.0625))
    q_h = quant(T.xh[:, XH_H:XH_H + 256], T.xhs[:, XH_H:XH_H + 256], T.ht[:], rel)
    for h in range(2):
        a = XH_H + 128 * h
        m_e = mm(T.pe[:, 512 * h:512 * h + 128], T.xh[:, a:a + 128], T.xhs[:, a:a + 128], T.mq[:], T.ms[:], True, True, q_h, q_m)
    m_row = mm(T.pe[:, 1024:1280], T.eq[:], T.es[:], T.xh[:, XH_H:XH_H + 256], T.xhs[:, XH_H:XH_H + 256], True, True, q_e)
    v_ta = tt(T.tv[:, 0:128], T.num[:, 0:128], T.tri[:], A.is_lt, g_num, k_tri)
    v_tb = tt(T.tv[:, 384:512], T.num[:, 128:256], T.tri[:], A.is_lt)
    v_tc = ts(T.tv[:, 256:384], T.num[:, 0:128], 127.5, A.is_lt, None, None)
    a_va = act(T.inv[:], T.num[:], AF.Sign, g_num, scale=-1.0, bias=127.5, accum_out=one("nI", 0))
    key = T.pe[:, 8:1024:512]
    f = 0.6 * 2.0 ** -23
    v_fe = ts(col["fe"], key, f, A.mult, None, None, m_e)
    v_n2 = ts(col["n2"], key, -f, A.mult, 1e-30, A.max)
    v_e8 = copy(col["e8"], key)
    v_sc = tt(col["sc"], col["fe"], col["n2"], A.max, v_n2)
    ac = []
    for h in range(2):
        ac.append(act(T.cc[:, 256 * h:256 * h + 256], T.tv[:, 256 * h:256 * h + 256], AF.Identity, v_sc, v_tc, k_tv0,
                      scale=one("sc", h), bias=one("e8", h)))
    v_ni = ts(one("nI", 1), one("nI", 0), -0.5, A.mult, 128.0, A.add, a_va)
    for h in range(2):
        v_r = scan(T.rr[:, 8 * h:8 * h + 8], T.d0[:, 0:8], T.pe[:, 512 * h:512 * h + 8], 0.0, A.add, A.max)
    v_co = ts(col["corr"], col["e8"], 0.0, A.is_gt, one("nI", 1), A.mult, v_ni)
    v_cc = ts(col["cc"], col["corr"], DF - 0.5, A.add, None, None, v_co)
    for h in range(2):
        a_f = act(T.js[:, 768 + 8 * h:776 + 8 * h], T.rr[:, 8 * h:8 * h + 8], AF.Sign, v_r, scale=-1.0, bias=T.rr[:, 8 * h + 7:8 * h + 8], accum_out=one("F", h))
    vl = []
    for h in range(2):
        vl.append(tt(T.lt[:, 256 * h:256 * h + 256], T.pe[:, 1024:1280], T.cc[:, 256 * h:256 * h + 256], A.is_lt, ac[h], m_row))
    a_a = act(T.js[:, 1024:1280], T.lt[:, 0:256], AF.Copy, vl[0], accum_out=one("A", 0))
    v_f2 = ts(col["F2"], col["F"], 2.0, A.mult, 8.0, A.add, a_f)
    v_a1 = total(one("A", 1), T.lt[:, 256:512], vl[1])
    v_v0 = ts(T.tvv[:, 0:1], one("A", 0), one("cc", 0), A.is_gt, one("F2", 0), A.add, a_a, v_cc, v_f2, k_tvv)
    v_v1 = ts(T.tvv[:, 32:33], one("A", 1), one("cc", 1), A.is_gt, one("F2", 1), A.add, v_a1)
    v_tv = turn(T.tvt[:], T.tvv[:], v_v0, v_v1)
    wait("p", [v_tv])
    b = [done("p", g.partition_broadcast(T.rowv[:, 64 * q:64 * q + 64], T.tvt[32 * q:32 * q + 1, 0:64], 128)) for q in range(4)]
    v_b2 = ts(T.b2v[:], T.num[:], 127.5, A.is_lt, cf["b2"], A.mult, k_b2)
    for q in range(4):
        for h in range(2):
            k = 128 * h + 32 * q
            v_m2 = tt(T.m2[:, k:k + 32], T.rowv[:, 64 * q + 32 * h:64 * q + 32 * h + 32], T.b2v[:, k:k + 32], A.is_equal, b[q], v_b2)
    v_c2 = scan(T.cum2[:], T.zrow[:], T.m2[:], 0.0, A.add, A.add, v_m2, k_zrow)
    acc = []
    for v in range(NS2):
        acc.append(act(T.js[:, 256 * v:256 * v + 256], T.cum2[:], AF.Sign, v_c2, k_th2, scale=-1.0, bias=T.th2[:, v:v + 1], accum_out=T.l2[:, v:v + 1]))
    v_p = ts(T.jv[:, 0:256], T.cum2[:], T.th2[:, NS2:NS2 + 1], A.is_le, 2.0, A.mult, v_c2, v_lx)
    v_p = total(T.l2v[:], T.jv[:, 0:256], v_p)
    v_p = ts(T.l2[:, NS2:NS2 + 1], T.l2v[:], -256.0, A.add, None, None, v_p)
    v_lx = tt(T.lx2[:], T.l2[:, 0:8].indirect(T.of2[:, 0:2]), T.mk2[:], A.add, acc, v_p, k_mk2, k_of2, k_l2)
    v_lt = turn(T.lt2[:], T.lx2[:], v_lx)
    v_m0 = tt(T.mn2[:, 0:8], T.lt2[:, 0:8], T.lt2[:, 8:16], A.min, v_lt)
    v_m1 = tt(T.mn2[:, 8:16], T.lt2[:, 16:24], T.lt2[:, 24:32], A.min)
    v_o0 = ts(T.off2[:, 0:16:2], T.mn2[:, 0:8], 0.5, A.mult, cf["h"], A.add, v_m0, c_h)
    v_o1 = ts(T.off2[:, 1:16:2], T.mn2[:, 8:16], 0.5, A.mult, cf["h"], A.add, v_m1)
    v_s2 = copy(T.s2c[:].bitcast(dt.uint32), T.xh[:].bitcast(dt.uint32).indirect(T.off2[:]), v_o1, ready, q_h, z2, z3)
    a_s2 = act(T.s2s[:], T.xhs[:].indirect(T.off2[:]), AF.Copy, v_o1, ready)
    v_w0 = ts(T.offw[:, 0:16:2], T.mn2[:, 0:8], 0.5, A.mult, 128.0, A.add)
    v_w1 = ts(T.offw[:, 1:16:2], T.mn2[:, 8:16], 0.5, A.mult, 128.0, A.add)
    v_wn = tt(T.wn[:, 0:256], T.num[:], T.s128[:], A.add, k_s128)
    v_wg = copy(T.wg[:], T.wn[:].indirect(T.offw[:]), v_wn, v_w1, k_wn)
    v_g0 = copy(T.wgp[:, 0:128:2], T.wg[:, 0:256:4], v_wg)
    v_g1 = copy(T.wgp[:, 1:128:2], T.wg[:, 1:256:4])
    runs = [(0, 0, 128)] if me else [(0, 16, 16), (16, 0, 16), (32, 32, 96)]
    d_wg, d_wo = [], []
    for to, fr, n in runs:
        d_wg.append(dma("y", T.wgd[to:to + n, 0], T.wgp[0:1, fr:fr + n], v_g1))
        d_wo.append(dma("s", T.lwd[me, to:to + n, 0], T.wgp[0:1, fr:fr + n], v_g1))
    send_stage("2", T.s2c, T.s2s, T.l2c, T.l2s, T.r2c, T.r2s, place, v_s2, a_s2, T.wgd[:], T.lwd[me], T.rl2[:], d_wg)

    ready = [("c2", n_in["c2"]), ("s2", n_in["s2"]), dz]
    out = (T.pz[:, 0:128], T.pw[:, 512:640])
    my = []
    for k in range(2):
        a = 128 * k
        mm(out[k], T.vxq[:], T.vxs[:], T.l2c[:, a:a + 128], T.l2s[:, a:a + 128], True, False, ready, q_vx, q_vh, rel)
        my.append(mm(out[k], T.vhq[:], T.vhs[:], T.l2c[:, a + 2:a + 130], T.l2s[:, a + 2:a + 130], False, True))
    a_hp = act(T.hps[:], T.l2s[:, 0:256].indirect(T.ofh[:]), AF.Copy, ready, k_ofh)
    v_hp = copy(T.hp[:].bitcast(dt.uint32), T.l2c[:, 0:256].bitcast(dt.uint32).indirect(T.ofh[:]), ready, k_ofh)
    for r in range(2):
        v_y = copy(T.ys[:, r:64:2], T.pz[:, r:128:4], my[0])
        a_y = act(T.ys[:, 64 + r:128:2], T.pw[:, 512 + r:640:4], AF.Copy, my[1])
    dma("y", T.oc[:, 0:512], T.hp[:].bitcast(dt.uint8), v_hp)
    for k in range(4):
        dma("y", T.osc[4 * k:4 * k + 4, 0:128], T.hps[32 * k:32 * k + 4, 0:128], a_hp)
    dma("y", T.y[:, 0:64], T.ys[:, 0:64], v_y)
    dma("s", T.y[:, 64:128], T.ys[:, 64:128], a_y)
    dma("s", T.who[0:1, 0:128], T.lwd[:, 16 * me:16 * me + 16, 0], ("n2", n_in["n2"]), d_wo)
    g.wait_ge(T.sem.sent, sent[0])
    wait("p", [(s, everything[s]) for s in everything])
